import numpy as np
import ml_dtypes


def mxq(x, axis, fmt="e4m3"):
    dtype, down = {"e4m3": (ml_dtypes.float8_e4m3fn, 7), "e5m2": (ml_dtypes.float8_e5m2, 14)}[fmt]
    v = np.moveaxis(np.asarray(x, np.float32).astype(ml_dtypes.bfloat16).astype(np.float64), axis, -1)
    blocks = v.reshape(v.shape[:-1] + (-1, 32))
    amax = np.abs(blocks).max(-1, keepdims=True)
    byte = np.maximum(np.where(amax > 0, np.frexp(amax)[1] - 1 + 127, 0) - down, 1)
    scale = np.exp2(byte - 127.0)
    codes = (blocks / scale).astype(np.float32).astype(dtype).astype(np.float64)
    return np.moveaxis((codes * scale).reshape(v.shape), -1, axis)


WIDE = False


def mx_kscale(k):
    if not WIDE:
        return np.ones(k)
    levels = np.array([10, -10, 5, -5, 0])
    if k % 512:
        return np.exp2(np.random.permutation(np.resize(levels, k // 32))).repeat(32)
    a = np.empty((k // 512, 16))
    for p in range(k // 512):
        a[p, :8] = np.random.permutation(np.resize(levels, 8))
        for g in range(8):
            far = levels[np.abs(levels - a[p, g]) >= 10]
            a[p, g + 8] = far[np.random.randint(len(far))]
    return np.exp2(a.ravel()).repeat(32)


def f64(x):
    return np.asarray(x).astype(np.float64)


def striped(idx):
    return np.tile(idx.reshape(-1, 16).T, (8, 1)).astype(np.uint16)


def unstriped(offs):
    return offs[:16].T.reshape(-1).astype(np.int64)


def pack_weight(w):
    k, n = w.shape
    w = f64(np.asarray(w, np.float32).astype(ml_dtypes.bfloat16)).reshape(k // 32, 32, n)
    amax = np.abs(w).max(1)
    byte = np.clip(np.where(amax > 0, np.frexp(amax)[1] - 1 + 127 - 7, 1), 1, 254)
    scaled = (w * np.exp2(127.0 - byte)[:, None, :]).reshape(k, n).astype(np.float32)
    words = np.ascontiguousarray(scaled.reshape(k // 512, 128, 4, n).transpose(0, 1, 3, 2)).astype(ml_dtypes.float8_e4m3fn).view(np.uint8)
    return words, np.ascontiguousarray(byte.astype(np.uint8).reshape(k // 512, 16, n))


def unpack_weight(words, scales):
    g, p, n, _ = words.shape
    vals = np.ascontiguousarray(words).view(ml_dtypes.float8_e4m3fn).astype(np.float64) * np.repeat(np.exp2(scales.astype(np.float64) - 127.0), 8, axis=1)[..., None]
    return vals.transpose(0, 1, 3, 2).reshape(g * 512, n)


def relu(v):
    return np.maximum(v, 0.0)


def gelu(v):
    return 0.5 * v * (1.0 + np.tanh(np.sqrt(2.0 / np.pi) * (v + 0.044715 * v**3)))


K, T, S, D, V, H, N, U = 512, 4096, 1024, 2, 512, 512, 128, 256
P = 2 ** 7


def setup_inputs():
    n = np.random.standard_normal
    s = mx_kscale(K)[:, None]
    u = mx_kscale(H)
    packed_xT = pack_weight(n((K, T)) * s)
    packed_w2 = pack_weight(n((H, N)) / np.sqrt(H) / u[:, None])
    return {
        "x_words": packed_xT[0],
        "x_scales": packed_xT[1],
        "w1": (n((K, H)) / np.sqrt(K) / s * u).astype(np.float32),
        "w2_words": packed_w2[0],
        "w2_scales": packed_w2[1],
        "gate": (np.tile(np.random.uniform(0.2, 1.0, (D, 1, V)) / np.sqrt(D), (1, P, 1))).astype(np.float32),
        "gate2": (np.tile(np.random.uniform(0.2, 1.0, (D, 1, U)) / np.sqrt(D), (1, P, 1))).astype(np.float32),
        "offs": striped(np.random.permutation(T)[:S]),
        "pos1": striped(np.random.permutation(S)[:V]),
        "pos2": striped(np.random.permutation(S)[:V]),
        "nxt1": striped(np.random.permutation(V)[:U]),
        "nxt2": striped(np.random.permutation(V)[:U]),
    }


def reference(x_words, x_scales, w1, w2_words, w2_scales, gate, gate2, offs, pos1, pos2, nxt1, nxt2):
    xq = unpack_weight(x_words, x_scales)[:, unstriped(offs)]
    h = gelu(mxq(f64(w1), 0, "e4m3").T @ xq)
    z = h[:, unstriped(pos1)] * f64(gate)[0, :1] + h[:, unstriped(pos2)] * f64(gate)[1, :1]
    g = relu(unpack_weight(w2_words, w2_scales).T @ mxq(z, 0, "e4m3"))
    return g[:, unstriped(nxt1)] * f64(gate2)[0, :1] + g[:, unstriped(nxt2)] * f64(gate2)[1, :1]

@@ -1,0 +1,156 @@
+from contextlib import ExitStack
+
+import concourse.mybir as mybir
+
+K, T, S, V, H, N, U = 512, 4096, 1024, 512, 512, 128, 256
+FLOPS = 2 * K * H * S + 2 * H * N * V
+
+F32 = mybir.dt.float32
+BF16 = mybir.dt.bfloat16
+I32 = mybir.dt.int32
+U32 = mybir.dt.uint32
+U16 = mybir.dt.uint16
+U8 = mybir.dt.uint8
+FP8X4 = mybir.dt.float8_e4m3fn_x4
+ACT = mybir.ActivationFunctionType
+ALU = mybir.AluOpType
+
+P = 128
+PACK = 4
+BANK = 512
+LIST = 16
+
+
+def load_scale_rows(queue, tile, rows):
+    for r in range(4):
+        queue.dma_start(out=tile[:].bitcast(I32)[r:P:32, :], in_=rows.bitcast(I32)[r:16:4, :])
+
+
+def tile_picked_hop2_gelu_p_kernel(
+    tc, x_words, x_scales, w1, w2_words, w2_scales, gate, gate2, offs, pos1, pos2, nxt1, nxt2, out
+):
+    nc = tc.nc
+    with ExitStack() as ctx:
+        lists = ctx.enter_context(tc.tile_pool(name="lists", bufs=1))
+        keep = ctx.enter_context(tc.tile_pool(name="keep", bufs=1))
+        psum = ctx.enter_context(tc.psum_pool(name="psum", bufs=4))
+        psum2 = ctx.enter_context(tc.psum_pool(name="psum2", bufs=2))
+
+        xs = keep.tile([P, T], U8, name="xs", align_bytes=64)
+        nc.vector.memset(xs[:].bitcast(I32), 0)
+        w2s = keep.tile([P, N], U8, name="w2s", align_bytes=64)
+        nc.vector.memset(w2s[:].bitcast(I32), 0)
+
+        offs_t = lists.tile([P, S // LIST], U16, name="offs_t")
+        nc.sync.dma_start(offs_t[:], offs)
+        xw = keep.tile([P, T], I32, name="xw", align_bytes=64)
+        nc.sync.dma_start(out=xw[:], in_=x_words[0].rearrange("p n t -> p (n t)").bitcast(I32))
+        load_scale_rows(nc.scalar, xs, x_scales[0])
+
+        w1_rows = w1.rearrange("(p j) c -> p j c", j=PACK)
+        w1_raw = []
+        for half in range(2):
+            raw = keep.tile([P, PACK, H // 2], F32, name="w1_raw%d" % half)
+            nc.sync.dma_start(out=raw[:], in_=w1_rows[:, :, half * 256 : (half + 1) * 256])
+            w1_raw.append(raw)
+
+        small = []
+        for name, src, n in (("pos1", pos1, V), ("pos2", pos2, V)):
+            t_ = lists.tile([P, n // LIST], U16, name=name + "_t")
+            nc.sync.dma_start(t_[:], src)
+            small.append(t_)
+        gates = []
+        for d in range(2):
+            gt = keep.tile([P, V], F32, name="gate%d" % d)
+            nc.sync.dma_start(out=gt[:], in_=gate[d])
+            gates.append(gt)
+        w2w = keep.tile([P, N], I32, name="w2w", align_bytes=64)
+        nc.sync.dma_start(out=w2w[:], in_=w2_words[0].rearrange("p n t -> p (n t)").bitcast(I32))
+        load_scale_rows(nc.sync, w2s, w2_scales[0])
+        for name, src, n in (("nxt1", nxt1, U), ("nxt2", nxt2, U)):
+            t_ = lists.tile([P, n // LIST], U16, name=name + "_t")
+            nc.sync.dma_start(t_[:], src)
+            small.append(t_)
+        gates2 = keep.tile([P, 2, U], F32, name="gates2")
+        nc.sync.dma_start(out=gates2[:], in_=gate2.rearrange("d p r -> p d r"))
+
+        warm = keep.tile([P, 1], F32, name="warm")
+        nc.gpsimd.memset(warm[:], 0.0)
+        warm2 = keep.tile([P, 1], F32, name="warm2")
+        nc.scalar.activation(warm2[:], warm[:], ACT.Gelu_apprx_tanh)
+
+        gs = keep.tile([P, S], U8, name="gs", align_bytes=64)
+        nc.vector.tensor_copy(gs[:], xs[:].indirect(offs_t[:]))
+        gw = []
+        for half in range(2):
+            g_ = keep.tile([P, BANK], U32, name="gw%d" % half, align_bytes=64)
+            nc.vector.tensor_copy(g_[:], xw[:].bitcast(U32).indirect(offs_t[:, half * 32 : (half + 1) * 32]))
+            gw.append(g_)
+
+        grouped = keep.tile([P, PACK * P * PACK], BF16, name="grouped", align_bytes=64)
+        gview = grouped[:].rearrange("p (t m j) -> p m j t", t=PACK, j=PACK)
+        nc.scalar.copy(gview[:, 0:64], w1_raw[0][:].rearrange("p j (m t) -> p m j t", t=PACK))
+        nc.vector.tensor_copy(gview[:, 64:128], w1_raw[1][:].rearrange("p j (m t) -> p m j t", t=PACK))
+
+        h = []
+        for t in range(PACK):
+            w1c = keep.tile([P, P], U32, name="w1c%d" % t, align_bytes=64)
+            w1s = keep.tile([P, P], U8, name="w1s%d" % t, align_bytes=64)
+            nc.vector.quantize_mx(out=w1c[:].bitcast(FP8X4), scales=w1s[:], in_=grouped[:, t * 512 : (t + 1) * 512])
+            ht = keep.tile([P, S], F32, name="h%d" % t)
+            for half in range(2):
+                acc = psum.tile([P, BANK], F32, name="acc")
+                nc.tensor.matmul_mx(
+                    out=acc[:], lhsT=w1c[:].bitcast(FP8X4), lhsT_scale=w1s[:],
+                    rhs=gw[half][:].bitcast(FP8X4), rhs_scale=gs[:, half * BANK : (half + 1) * BANK],
+                    start=True, stop=True,
+                )
+                nc.scalar.activation(ht[:, half * BANK : (half + 1) * BANK], acc[:], ACT.Gelu_apprx_tanh)
+            h.append(ht)
+
+        terms = [[keep.tile([P, PACK, 256], F32, name="term%d%d" % (d, half)) for half in range(2)] for d in range(2)]
+        g = keep.tile([P, V], F32, name="g")
+        zb = [keep.tile([P, 256 * PACK], BF16, name="zb%d" % half, align_bytes=64) for half in range(2)]
+        zc = [keep.tile([P, 256], U32, name="zc%d" % half, align_bytes=64) for half in range(2)]
+        zs = [keep.tile([P, 256], U8, name="zs%d" % half, align_bytes=64) for half in range(2)]
+
+        def gather(t, half):
+            cols = slice(half * 256, (half + 1) * 256)
+            for d in range(2):
+                nc.vector.tensor_tensor(
+                    terms[d][half][:, t, :], h[t][:].indirect(small[d][:, half * 16 : (half + 1) * 16]), gates[d][:, cols], ALU.mult
+                )
+
+        def add(half):
+            nc.vector.tensor_tensor(
+                zb[half][:].rearrange("p (c i t) -> p c t i", i=4, t=PACK),
+                terms[0][half][:].rearrange("p t (c i) -> p c t i", i=4),
+                terms[1][half][:].rearrange("p t (c i) -> p c t i", i=4),
+                ALU.add,
+            )
+
+        def quant(half):
+            nc.vector.quantize_mx(out=zc[half][:].bitcast(FP8X4), scales=zs[half][:], in_=zb[half][:])
+            acc2 = psum2.tile([P, 256], F32, name="acc2")
+            nc.tensor.matmul_mx(
+                out=acc2[:], lhsT=w2w[:].bitcast(FP8X4), lhsT_scale=w2s[:],
+                rhs=zc[half][:].bitcast(FP8X4), rhs_scale=zs[half][:], start=True, stop=True,
+            )
+            nc.scalar.activation(g[:, half * 256 : (half + 1) * 256], acc2[:], ACT.Relu)
+
+        for t in range(3):
+            for half in range(2):
+                gather(t, half)
+        gather(3, 0)
+        add(0)
+        gather(3, 1)
+        quant(0)
+        add(1)
+        quant(1)
+
+        o = [keep.tile([P, U], F32, name="o%d" % d) for d in range(2)]
+        for d in range(2):
+            nc.vector.tensor_tensor(o[d][:], g[:].indirect(small[2 + d][:]), gates2[:, d, :], ALU.mult)
+        res = keep.tile([P, U], F32, name="res")
+        nc.vector.tensor_tensor(res[:], o[0][:], o[1][:], ALU.add)
+        nc.sync.dma_start(out=out, in_=res[:])

@@ -1,6 +1,7 @@
 from contextlib import ExitStack
 
 import concourse.mybir as mybir
+from concourse.masks import make_identity
 
 K, T, S, V, H, N, U = 512, 4096, 1024, 512, 512, 128, 256
 FLOPS = 2 * K * H * S + 2 * H * N * V
@@ -19,6 +20,8 @@ P = 128
 PACK = 4
 BANK = 512
 LIST = 16
+TURNED = 3
+GROUPS = ((0, 1), (2,), (3,))
 
 
 def load_scale_rows(queue, tile, rows):
@@ -34,36 +37,41 @@ def tile_picked_hop2_gelu_p_kernel(
         lists = ctx.enter_context(tc.tile_pool(name="lists", bufs=1))
         keep = ctx.enter_context(tc.tile_pool(name="keep", bufs=1))
         psum = ctx.enter_context(tc.psum_pool(name="psum", bufs=4))
-        psum2 = ctx.enter_context(tc.psum_pool(name="psum2", bufs=2))
 
         xs = keep.tile([P, T], U8, name="xs", align_bytes=64)
-        nc.vector.memset(xs[:].bitcast(I32), 0)
+        nc.gpsimd.memset(xs[:].bitcast(I32)[:, 0:512], 0)
+        nc.vector.memset(xs[:].bitcast(I32)[:, 512:1024], 0)
         w2s = keep.tile([P, N], U8, name="w2s", align_bytes=64)
         nc.vector.memset(w2s[:].bitcast(I32), 0)
+        gate_rows = keep.tile([P, P], F32, name="gate_rows")
+        nc.gpsimd.memset(gate_rows[:], 0.0)
+        ident = keep.tile([P, P], F32, name="ident")
+        make_identity(nc, ident[:])
 
         offs_t = lists.tile([P, S // LIST], U16, name="offs_t")
         nc.sync.dma_start(offs_t[:], offs)
+        w1_rows = w1.rearrange("(p j) c -> p j c", j=PACK)
+        cuts = (0, 128, 384, 512)
+        w1_raw = [keep.tile([P, PACK, cuts[i + 1] - cuts[i]], F32, name="w1_raw%d" % i) for i in range(3)]
+        nc.sync.dma_start(out=w1_raw[0][:], in_=w1_rows[:, :, cuts[0] : cuts[1]])
+        small = []
+        t_ = lists.tile([P, V // LIST], U16, name="pos1_t")
+        nc.sync.dma_start(t_[:], pos1)
+        small.append(t_)
+        load_scale_rows(nc.sync, xs, x_scales[0])
         xw = keep.tile([P, T], I32, name="xw", align_bytes=64)
         nc.sync.dma_start(out=xw[:], in_=x_words[0].rearrange("p n t -> p (n t)").bitcast(I32))
-        load_scale_rows(nc.scalar, xs, x_scales[0])
+        for i in (1, 2):
+            nc.sync.dma_start(out=w1_raw[i][:], in_=w1_rows[:, :, cuts[i] : cuts[i + 1]])
 
-        w1_rows = w1.rearrange("(p j) c -> p j c", j=PACK)
-        w1_raw = []
-        for half in range(2):
-            raw = keep.tile([P, PACK, H // 2], F32, name="w1_raw%d" % half)
-            nc.sync.dma_start(out=raw[:], in_=w1_rows[:, :, half * 256 : (half + 1) * 256])
-            w1_raw.append(raw)
-
-        small = []
-        for name, src, n in (("pos1", pos1, V), ("pos2", pos2, V)):
+        for name, src, n in (("pos2", pos2, V),):
             t_ = lists.tile([P, n // LIST], U16, name=name + "_t")
             nc.sync.dma_start(t_[:], src)
             small.append(t_)
-        gates = []
         for d in range(2):
-            gt = keep.tile([P, V], F32, name="gate%d" % d)
-            nc.sync.dma_start(out=gt[:], in_=gate[d])
-            gates.append(gt)
+            nc.sync.dma_start(out=gate_rows[4 * d : 4 * d + 4, :], in_=gate[d, 0, :].rearrange("(c p) -> c p", p=P))
+        gate_last = keep.tile([P, 2, P], F32, name="gate_last")
+        nc.sync.dma_start(out=gate_last[:], in_=gate[:, :, TURNED * P :].rearrange("d p v -> p d v"))
         w2w = keep.tile([P, N], I32, name="w2w", align_bytes=64)
         nc.sync.dma_start(out=w2w[:], in_=w2_words[0].rearrange("p n t -> p (n t)").bitcast(I32))
         load_scale_rows(nc.sync, w2s, w2_scales[0])
@@ -75,9 +83,7 @@ def tile_picked_hop2_gelu_p_kernel(
         nc.sync.dma_start(out=gates2[:], in_=gate2.rearrange("d p r -> p d r"))
 
         warm = keep.tile([P, 1], F32, name="warm")
-        nc.gpsimd.memset(warm[:], 0.0)
-        warm2 = keep.tile([P, 1], F32, name="warm2")
-        nc.scalar.activation(warm2[:], warm[:], ACT.Gelu_apprx_tanh)
+        nc.scalar.activation(warm[:], ident[:, 0:1], ACT.Gelu_apprx_tanh)
 
         gs = keep.tile([P, S], U8, name="gs", align_bytes=64)
         nc.vector.tensor_copy(gs[:], xs[:].indirect(offs_t[:]))
@@ -87,19 +93,29 @@ def tile_picked_hop2_gelu_p_kernel(
             nc.vector.tensor_copy(g_[:], xw[:].bitcast(U32).indirect(offs_t[:, half * 32 : (half + 1) * 32]))
             gw.append(g_)
 
-        grouped = keep.tile([P, PACK * P * PACK], BF16, name="grouped", align_bytes=64)
-        gview = grouped[:].rearrange("p (t m j) -> p m j t", t=PACK, j=PACK)
-        nc.scalar.copy(gview[:, 0:64], w1_raw[0][:].rearrange("p j (m t) -> p m j t", t=PACK))
-        nc.vector.tensor_copy(gview[:, 64:128], w1_raw[1][:].rearrange("p j (m t) -> p m j t", t=PACK))
+        first = keep.tile([P, P * PACK], BF16, name="first", tag="grouped", align_bytes=64)
+        for i in range(3):
+            nc.scalar.copy(
+                first[:].rearrange("p (m j) -> p m j", j=PACK)[:, cuts[i] // 4 : cuts[i + 1] // 4],
+                w1_raw[i][:].rearrange("p j (m t) -> p m j t", t=PACK)[:, :, :, 0],
+            )
 
         h = []
         for t in range(PACK):
+            if t == 1:
+                rest = keep.tile([P, 3 * P * PACK], BF16, name="rest", tag="grouped", align_bytes=64)
+                for i in range(3):
+                    nc.vector.tensor_copy(
+                        rest[:].rearrange("p (t m j) -> p m j t", t=3, j=PACK)[:, cuts[i] // 4 : cuts[i + 1] // 4],
+                        w1_raw[i][:].rearrange("p j (m t) -> p m j t", t=PACK)[:, :, :, 1:],
+                    )
             w1c = keep.tile([P, P], U32, name="w1c%d" % t, align_bytes=64)
             w1s = keep.tile([P, P], U8, name="w1s%d" % t, align_bytes=64)
-            nc.vector.quantize_mx(out=w1c[:].bitcast(FP8X4), scales=w1s[:], in_=grouped[:, t * 512 : (t + 1) * 512])
+            source = first[:] if t == 0 else rest[:, (t - 1) * 512 : t * 512]
+            nc.vector.quantize_mx(out=w1c[:].bitcast(FP8X4), scales=w1s[:], in_=source)
             ht = keep.tile([P, S], F32, name="h%d" % t)
             for half in range(2):
-                acc = psum.tile([P, BANK], F32, name="acc")
+                acc = psum.tile([P, BANK], F32, name="acc", tag="acc")
                 nc.tensor.matmul_mx(
                     out=acc[:], lhsT=w1c[:].bitcast(FP8X4), lhsT_scale=w1s[:],
                     rhs=gw[half][:].bitcast(FP8X4), rhs_scale=gs[:, half * BANK : (half + 1) * BANK],
@@ -108,45 +124,71 @@ def tile_picked_hop2_gelu_p_kernel(
                 nc.scalar.activation(ht[:, half * BANK : (half + 1) * BANK], acc[:], ACT.Gelu_apprx_tanh)
             h.append(ht)
 
-        terms = [[keep.tile([P, PACK, 256], F32, name="term%d%d" % (d, half)) for half in range(2)] for d in range(2)]
-        g = keep.tile([P, V], F32, name="g")
-        zb = [keep.tile([P, 256 * PACK], BF16, name="zb%d" % half, align_bytes=64) for half in range(2)]
-        zc = [keep.tile([P, 256], U32, name="zc%d" % half, align_bytes=64) for half in range(2)]
-        zs = [keep.tile([P, 256], U8, name="zs%d" % half, align_bytes=64) for half in range(2)]
+        gate_ps = psum.tile([P, P], F32, name="gate_ps", tag="acc")
+        nc.tensor.transpose(gate_ps[:], gate_rows[:], ident[:])
+        gate_col = keep.tile([P, 8], F32, name="gate_col")
+        nc.scalar.copy(gate_col[:], gate_ps[:, 0:8])
 
-        def gather(t, half):
-            cols = slice(half * 256, (half + 1) * 256)
+        zsum = [psum.tile([P, PACK, P], F32, name="zsum%d" % b, tag="acc") for b in range(TURNED)]
+        picked = {}
+        for group in GROUPS:
+            for t in group:
+                if t < PACK - 1:
+                    for d in range(2):
+                        pk = keep.tile([P, TURNED * P], F32, name="pk%d%d" % (t, d))
+                        nc.vector.tensor_copy(pk[:], h[t][:].indirect(small[d][:, 0 : TURNED * 8]))
+                        for b in range(TURNED):
+                            picked[t, d, b] = pk[:, b * P : (b + 1) * P]
+                else:
+                    for b in range(TURNED):
+                        for d in range(2):
+                            pk = keep.tile([P, P], F32, name="pk%d%d%d" % (t, d, b), tag="late%d%d" % (d, b))
+                            nc.vector.tensor_copy(pk[:], h[t][:].indirect(small[d][:, b * 8 : (b + 1) * 8]))
+                            picked[t, d, b] = pk[:]
+            width = len(group) * P
+            for b in range(TURNED):
+                turned = psum.tile([P, 2, width], F32, name="turned", tag="turned")
+                for d in range(2):
+                    for i, t in enumerate(group):
+                        nc.tensor.transpose(turned[:, d, i * P : (i + 1) * P], picked[t, d, b], ident[:])
+                gated = keep.tile([P, 2, width], F32, name="gated%d%d" % (group[0], b))
+                for d in range(2):
+                    nc.scalar.activation(gated[:, d, :], turned[:, d, :], ACT.Copy, scale=gate_col[:, 4 * d + b : 4 * d + b + 1])
+                for i, t in enumerate(group):
+                    for d in range(2):
+                        nc.tensor.matmul(
+                            zsum[b][:, t, :], gated[:, d, i * P : (i + 1) * P], ident[:],
+                            start=(d == 0), stop=(d == 1), is_transpose=True,
+                        )
+
+        zb = [keep.tile([P, P * PACK], BF16, name="zb%d" % b, align_bytes=64) for b in range(4)]
+        for b in range(TURNED):
+            nc.scalar.copy(zb[b][:].rearrange("p (v t) -> p v t", t=PACK), zsum[b][:].rearrange("p t v -> p v t"))
+
+        terms = [keep.tile([P, PACK, P], F32, name="term%d" % d, tag="late%d0" % d) for d in range(2)]
+        for t in range(PACK):
             for d in range(2):
                 nc.vector.tensor_tensor(
-                    terms[d][half][:, t, :], h[t][:].indirect(small[d][:, half * 16 : (half + 1) * 16]), gates[d][:, cols], ALU.mult
+                    terms[d][:, t, :], h[t][:].indirect(small[d][:, TURNED * 8 :]), gate_last[:, d, :], ALU.mult
                 )
+        nc.vector.tensor_tensor(
+            zb[TURNED][:].rearrange("p (c i t) -> p c t i", i=4, t=PACK),
+            terms[0][:].rearrange("p t (c i) -> p c t i", i=4),
+            terms[1][:].rearrange("p t (c i) -> p c t i", i=4),
+            ALU.add,
+        )
 
-        def add(half):
-            nc.vector.tensor_tensor(
-                zb[half][:].rearrange("p (c i t) -> p c t i", i=4, t=PACK),
-                terms[0][half][:].rearrange("p t (c i) -> p c t i", i=4),
-                terms[1][half][:].rearrange("p t (c i) -> p c t i", i=4),
-                ALU.add,
-            )
-
-        def quant(half):
-            nc.vector.quantize_mx(out=zc[half][:].bitcast(FP8X4), scales=zs[half][:], in_=zb[half][:])
-            acc2 = psum2.tile([P, 256], F32, name="acc2")
+        g = keep.tile([P, V], F32, name="g")
+        for b in range(4):
+            zc = keep.tile([P, P], U32, name="zc%d" % b, align_bytes=64)
+            zs = keep.tile([P, P], U8, name="zs%d" % b, align_bytes=64)
+            nc.vector.quantize_mx(out=zc[:].bitcast(FP8X4), scales=zs[:], in_=zb[b][:])
+            acc2 = psum.tile([P, P], F32, name="acc2", tag="turned")
             nc.tensor.matmul_mx(
                 out=acc2[:], lhsT=w2w[:].bitcast(FP8X4), lhsT_scale=w2s[:],
-                rhs=zc[half][:].bitcast(FP8X4), rhs_scale=zs[half][:], start=True, stop=True,
+                rhs=zc[:].bitcast(FP8X4), rhs_scale=zs[:], start=True, stop=True,
             )
-            nc.scalar.activation(g[:, half * 256 : (half + 1) * 256], acc2[:], ACT.Relu)
-
-        for t in range(3):
-            for half in range(2):
-                gather(t, half)
-        gather(3, 0)
-        add(0)
-        gather(3, 1)
-        quant(0)
-        add(1)
-        quant(1)
+            nc.scalar.activation(g[:, b * P : (b + 1) * P], acc2[:], ACT.Relu)
 
         o = [keep.tile([P, U], F32, name="o%d" % d) for d in range(2)]
         for d in range(2):

@@ -43,8 +43,6 @@ def tile_picked_hop2_gelu_p_kernel(
         nc.vector.memset(xs[:].bitcast(I32)[:, 512:1024], 0)
         w2s = keep.tile([P, N], U8, name="w2s", align_bytes=64)
         nc.vector.memset(w2s[:].bitcast(I32), 0)
-        gate_rows = keep.tile([P, P], F32, name="gate_rows")
-        nc.gpsimd.memset(gate_rows[:], 0.0)
         ident = keep.tile([P, P], F32, name="ident")
         make_identity(nc, ident[:])
 
@@ -68,10 +66,9 @@ def tile_picked_hop2_gelu_p_kernel(
             t_ = lists.tile([P, n // LIST], U16, name=name + "_t")
             nc.sync.dma_start(t_[:], src)
             small.append(t_)
+        gates = [keep.tile([P, V], F32, name="gate%d" % d) for d in range(2)]
         for d in range(2):
-            nc.sync.dma_start(out=gate_rows[4 * d : 4 * d + 4, :], in_=gate[d, 0, :].rearrange("(c p) -> c p", p=P))
-        gate_last = keep.tile([P, 2, P], F32, name="gate_last")
-        nc.sync.dma_start(out=gate_last[:], in_=gate[:, :, TURNED * P :].rearrange("d p v -> p d v"))
+            nc.sync.dma_start(out=gates[d][:], in_=gate[d])
         w2w = keep.tile([P, N], I32, name="w2w", align_bytes=64)
         nc.sync.dma_start(out=w2w[:], in_=w2_words[0].rearrange("p n t -> p (n t)").bitcast(I32))
         load_scale_rows(nc.sync, w2s, w2_scales[0])
@@ -114,85 +111,97 @@ def tile_picked_hop2_gelu_p_kernel(
             source = first[:] if t == 0 else rest[:, (t - 1) * 512 : t * 512]
             nc.vector.quantize_mx(out=w1c[:].bitcast(FP8X4), scales=w1s[:], in_=source)
             ht = keep.tile([P, S], F32, name="h%d" % t)
-            for half in range(2):
-                acc = psum.tile([P, BANK], F32, name="acc", tag="acc")
+            width = 256 if t == 0 else BANK
+            for start in range(0, S, width):
+                acc = psum.tile([P, width], F32, name="acc", tag="acc")
                 nc.tensor.matmul_mx(
                     out=acc[:], lhsT=w1c[:].bitcast(FP8X4), lhsT_scale=w1s[:],
-                    rhs=gw[half][:].bitcast(FP8X4), rhs_scale=gs[:, half * BANK : (half + 1) * BANK],
+                    rhs=gw[start // BANK][:, start % BANK : start % BANK + width].bitcast(FP8X4),
+                    rhs_scale=gs[:, start : start + width],
                     start=True, stop=True,
                 )
-                nc.scalar.activation(ht[:, half * BANK : (half + 1) * BANK], acc[:], ACT.Gelu_apprx_tanh)
+                nc.scalar.activation(ht[:, start : start + width], acc[:], ACT.Gelu_apprx_tanh)
             h.append(ht)
 
-        gate_ps = psum.tile([P, P], F32, name="gate_ps", tag="acc")
-        nc.tensor.transpose(gate_ps[:], gate_rows[:], ident[:])
-        gate_col = keep.tile([P, 8], F32, name="gate_col")
-        nc.scalar.copy(gate_col[:], gate_ps[:, 0:8])
-
-        zsum = [psum.tile([P, PACK, P], F32, name="zsum%d" % b, tag="acc") for b in range(TURNED)]
         picked = {}
-        for group in GROUPS:
-            for t in group:
+        words = [psum.tile([P, 2, P], F32, name="words%d" % b, tag="acc") for b in range(TURNED)]
+        for u in range(2):
+            for t in (2 * u, 2 * u + 1):
                 if t < PACK - 1:
                     for d in range(2):
                         pk = keep.tile([P, TURNED * P], F32, name="pk%d%d" % (t, d))
-                        nc.vector.tensor_copy(pk[:], h[t][:].indirect(small[d][:, 0 : TURNED * 8]))
+                        nc.vector.tensor_tensor(
+                            pk[:], h[t][:].indirect(small[d][:, 0 : TURNED * 8]), gates[d][:, 0 : TURNED * P], ALU.mult
+                        )
                         for b in range(TURNED):
                             picked[t, d, b] = pk[:, b * P : (b + 1) * P]
                 else:
                     for b in range(TURNED):
                         for d in range(2):
                             pk = keep.tile([P, P], F32, name="pk%d%d%d" % (t, d, b), tag="late%d%d" % (d, b))
-                            nc.vector.tensor_copy(pk[:], h[t][:].indirect(small[d][:, b * 8 : (b + 1) * 8]))
+                            nc.vector.tensor_tensor(
+                                pk[:], h[t][:].indirect(small[d][:, b * 8 : (b + 1) * 8]),
+                                gates[d][:, b * P : (b + 1) * P], ALU.mult,
+                            )
                             picked[t, d, b] = pk[:]
-            width = len(group) * P
             for b in range(TURNED):
-                turned = psum.tile([P, 2, width], F32, name="turned", tag="turned")
-                for d in range(2):
-                    for i, t in enumerate(group):
-                        nc.tensor.transpose(turned[:, d, i * P : (i + 1) * P], picked[t, d, b], ident[:])
-                gated = keep.tile([P, 2, width], F32, name="gated%d%d" % (group[0], b))
-                for d in range(2):
-                    nc.scalar.activation(gated[:, d, :], turned[:, d, :], ACT.Copy, scale=gate_col[:, 4 * d + b : 4 * d + b + 1])
-                for i, t in enumerate(group):
+                turned = psum.tile([P, 2, P], F32, name="turned", tag="turned")
+                for e in range(2):
                     for d in range(2):
                         nc.tensor.matmul(
-                            zsum[b][:, t, :], gated[:, d, i * P : (i + 1) * P], ident[:],
+                            turned[:, e, :], picked[2 * u + e, d, b], ident[:],
                             start=(d == 0), stop=(d == 1), is_transpose=True,
                         )
+                pairs = keep.tile([P, 2 * P], BF16, name="pairs%d%d" % (u, b), align_bytes=64)
+                nc.scalar.copy(pairs[:].rearrange("v (p e) -> v p e", e=2), turned[:].rearrange("v e p -> v p e"))
+                nc.tensor.transpose(words[b][:, u, :], pairs[:].bitcast(F32), ident[:])
 
-        zb = [keep.tile([P, P * PACK], BF16, name="zb%d" % b, align_bytes=64) for b in range(4)]
+        zb01 = keep.tile([P, 2 * P * PACK], BF16, name="zb01", tag="zb01", align_bytes=64)
+        zb2 = keep.tile([P, P * PACK], BF16, name="zb2", align_bytes=64)
         for b in range(TURNED):
-            nc.scalar.copy(zb[b][:].rearrange("p (v t) -> p v t", t=PACK), zsum[b][:].rearrange("p t v -> p v t"))
+            target = zb01[:, b * 512 : (b + 1) * 512] if b < 2 else zb2[:]
+            nc.scalar.copy(target.bitcast(F32).rearrange("p (v u) -> p v u", u=2), words[b][:].rearrange("p u v -> p v u"))
 
         terms = [keep.tile([P, PACK, P], F32, name="term%d" % d, tag="late%d0" % d) for d in range(2)]
         for t in range(PACK):
             for d in range(2):
                 nc.vector.tensor_tensor(
-                    terms[d][:, t, :], h[t][:].indirect(small[d][:, TURNED * 8 :]), gate_last[:, d, :], ALU.mult
+                    terms[d][:, t, :], h[t][:].indirect(small[d][:, TURNED * 8 :]), gates[d][:, TURNED * P :], ALU.mult
                 )
-        nc.vector.tensor_tensor(
-            zb[TURNED][:].rearrange("p (c i t) -> p c t i", i=4, t=PACK),
-            terms[0][:].rearrange("p t (c i) -> p c t i", i=4),
-            terms[1][:].rearrange("p t (c i) -> p c t i", i=4),
-            ALU.add,
-        )
 
         g = keep.tile([P, V], F32, name="g")
-        for b in range(4):
-            zc = keep.tile([P, P], U32, name="zc%d" % b, align_bytes=64)
-            zs = keep.tile([P, P], U8, name="zs%d" % b, align_bytes=64)
-            nc.vector.quantize_mx(out=zc[:].bitcast(FP8X4), scales=zs[:], in_=zb[b][:])
-            acc2 = psum.tile([P, P], F32, name="acc2", tag="turned")
+
+        def second_layer(zb, start, width):
+            zc = keep.tile([P, width], U32, name="zc%d" % start, align_bytes=64)
+            zs = keep.tile([P, width], U8, name="zs%d" % start, align_bytes=64)
+            nc.vector.quantize_mx(out=zc[:].bitcast(FP8X4), scales=zs[:], in_=zb[:])
+            acc2 = psum.tile([P, width], F32, name="acc2", tag="turned")
             nc.tensor.matmul_mx(
                 out=acc2[:], lhsT=w2w[:].bitcast(FP8X4), lhsT_scale=w2s[:],
                 rhs=zc[:].bitcast(FP8X4), rhs_scale=zs[:], start=True, stop=True,
             )
-            nc.scalar.activation(g[:, b * P : (b + 1) * P], acc2[:], ACT.Relu)
+            nc.scalar.activation(g[:, start : start + width], acc2[:], ACT.Relu)
 
-        o = [keep.tile([P, U], F32, name="o%d" % d) for d in range(2)]
-        for d in range(2):
-            nc.vector.tensor_tensor(o[d][:], g[:].indirect(small[2 + d][:]), gates2[:, d, :], ALU.mult)
-        res = keep.tile([P, U], F32, name="res")
-        nc.vector.tensor_tensor(res[:], o[0][:], o[1][:], ALU.add)
-        nc.sync.dma_start(out=out, in_=res[:])
+        second_layer(zb01, 0, 256)
+        zb3 = keep.tile([P, P * PACK], BF16, name="zb3", tag="zb01", align_bytes=64)
+        nc.vector.tensor_tensor(
+            zb3[:].rearrange("p (c i t) -> p c t i", i=4, t=PACK),
+            terms[0][:].rearrange("p t (c i) -> p c t i", i=4),
+            terms[1][:].rearrange("p t (c i) -> p c t i", i=4),
+            ALU.add,
+        )
+        second_layer(zb2, 256, 128)
+        second_layer(zb3, 384, 128)
+
+        half = U // 2
+        o = [[keep.tile([P, half], F32, name="o%d%d" % (d, i)) for d in range(2)] for i in range(2)]
+        for i in range(2):
+            for d in range(2):
+                nc.vector.tensor_tensor(
+                    o[i][d][:], g[:].indirect(small[2 + d][:, 8 * i : 8 * i + 8]),
+                    gates2[:, d, half * i : half * (i + 1)], ALU.mult,
+                )
+        for i in range(2):
+            res = keep.tile([P, half], F32, name="res%d" % i)
+            nc.vector.tensor_tensor(res[:], o[i][0][:], o[i][1][:], ALU.add)
+            nc.sync.dma_start(out=out[:, half * i : half * (i + 1)], in_=res[:])

@@ -38,57 +38,54 @@ def tile_picked_hop2_gelu_p_kernel(
         keep = ctx.enter_context(tc.tile_pool(name="keep", bufs=1))
         psum = ctx.enter_context(tc.psum_pool(name="psum", bufs=4))
 
-        xs = keep.tile([P, T], U8, name="xs", align_bytes=64)
-        nc.gpsimd.memset(xs[:].bitcast(I32)[:, 0:512], 0)
-        nc.vector.memset(xs[:].bitcast(I32)[:, 512:1024], 0)
-        w2s = keep.tile([P, N], U8, name="w2s", align_bytes=64)
-        nc.vector.memset(w2s[:].bitcast(I32), 0)
+        xs = keep.tile([P, T], U8, name="xs", tag="xs", align_bytes=64)
+        nc.vector.memset(xs[:].bitcast(I32), 0)
         ident = keep.tile([P, P], F32, name="ident")
-        make_identity(nc, ident[:])
+        nc.vector.memset(ident[:], 0.0)
+        make_identity(nc, ident[:], nomemset=True)
+        gs = keep.tile([P, S], U8, name="gs", align_bytes=64)
+        nc.vector.memset(gs[:].bitcast(I32), 0)
 
         offs_t = lists.tile([P, S // LIST], U16, name="offs_t")
         nc.sync.dma_start(offs_t[:], offs)
         w1_rows = w1.rearrange("(p j) c -> p j c", j=PACK)
         cuts = (0, 128, 384, 512)
-        w1_raw = [keep.tile([P, PACK, cuts[i + 1] - cuts[i]], F32, name="w1_raw%d" % i) for i in range(3)]
+        w1_raw = [
+            keep.tile([P, PACK, cuts[i + 1] - cuts[i]], F32, name="w1_raw%d" % i, tag="w1_raw%d" % i) for i in range(3)
+        ]
         nc.sync.dma_start(out=w1_raw[0][:], in_=w1_rows[:, :, cuts[0] : cuts[1]])
         small = []
-        t_ = lists.tile([P, V // LIST], U16, name="pos1_t")
-        nc.sync.dma_start(t_[:], pos1)
-        small.append(t_)
-        load_scale_rows(nc.sync, xs, x_scales[0])
-        xw = keep.tile([P, T], I32, name="xw", align_bytes=64)
+        for name, src, n in (("pos1", pos1, V), ("pos2", pos2, V), ("nxt1", nxt1, U), ("nxt2", nxt2, U)):
+            t_ = lists.tile([P, n // LIST], U16, name=name + "_t")
+            nc.sync.dma_start(t_[:], src)
+            small.append(t_)
+        nc.sync.dma_start(out=xs[:].bitcast(I32)[0:P:8, :], in_=x_scales[0].bitcast(I32))
+        xw = keep.tile([P, T], I32, name="xw", tag="xw", align_bytes=64)
         nc.sync.dma_start(out=xw[:], in_=x_words[0].rearrange("p n t -> p (n t)").bitcast(I32))
         for i in (1, 2):
             nc.sync.dma_start(out=w1_raw[i][:], in_=w1_rows[:, :, cuts[i] : cuts[i + 1]])
 
-        for name, src, n in (("pos2", pos2, V),):
-            t_ = lists.tile([P, n // LIST], U16, name=name + "_t")
-            nc.sync.dma_start(t_[:], src)
-            small.append(t_)
-        gates = [keep.tile([P, V], F32, name="gate%d" % d) for d in range(2)]
-        for d in range(2):
-            nc.sync.dma_start(out=gates[d][:], in_=gate[d])
-        w2w = keep.tile([P, N], I32, name="w2w", align_bytes=64)
-        nc.sync.dma_start(out=w2w[:], in_=w2_words[0].rearrange("p n t -> p (n t)").bitcast(I32))
-        load_scale_rows(nc.sync, w2s, w2_scales[0])
-        for name, src, n in (("nxt1", nxt1, U), ("nxt2", nxt2, U)):
-            t_ = lists.tile([P, n // LIST], U16, name=name + "_t")
-            nc.sync.dma_start(t_[:], src)
-            small.append(t_)
-        gates2 = keep.tile([P, 2, U], F32, name="gates2")
-        nc.sync.dma_start(out=gates2[:], in_=gate2.rearrange("d p r -> p d r"))
-
         warm = keep.tile([P, 1], F32, name="warm")
         nc.scalar.activation(warm[:], ident[:, 0:1], ACT.Gelu_apprx_tanh)
 
-        gs = keep.tile([P, S], U8, name="gs", align_bytes=64)
-        nc.vector.tensor_copy(gs[:], xs[:].indirect(offs_t[:]))
+        gs_raw = keep.tile([P, S], U8, name="gs_raw", tag="gs_raw", align_bytes=64)
+        nc.vector.tensor_copy(gs_raw[:], xs[:].indirect(offs_t[:]))
+        for r in range(4):
+            nc.scalar.dma_start(out=gs[:].bitcast(I32)[r:P:32, :], in_=gs_raw[:].bitcast(I32)[8 * r : P : 32, :])
+        gate_t = keep.tile([P, 2, V], F32, name="gate_t", tag="xs", align_bytes=64)
+        nc.sync.dma_start(out=gate_t[:], in_=gate.rearrange("d p v -> p d v"))
+        gates = [gate_t[:, d, :] for d in range(2)]
+        w2w = keep.tile([P, N], I32, name="w2w", tag="gs_raw", align_bytes=64)
+        nc.sync.dma_start(out=w2w[:], in_=w2_words[0].rearrange("p n t -> p (n t)").bitcast(I32))
         gw = []
         for half in range(2):
             g_ = keep.tile([P, BANK], U32, name="gw%d" % half, align_bytes=64)
             nc.vector.tensor_copy(g_[:], xw[:].bitcast(U32).indirect(offs_t[:, half * 32 : (half + 1) * 32]))
             gw.append(g_)
+
+        w2s = keep.tile([P, N], U8, name="w2s", tag="xw", align_bytes=64)
+        nc.vector.memset(w2s[:].bitcast(I32), 0)
+        load_scale_rows(nc.sync, w2s, w2_scales[0])
 
         first = keep.tile([P, P * PACK], BF16, name="first", tag="grouped", align_bytes=64)
         for i in range(3):
@@ -122,6 +119,9 @@ def tile_picked_hop2_gelu_p_kernel(
                 )
                 nc.scalar.activation(ht[:, start : start + width], acc[:], ACT.Gelu_apprx_tanh)
             h.append(ht)
+
+        gates2 = keep.tile([P, 2, U], F32, name="gates2", tag="w1_raw0")
+        nc.sync.dma_start(out=gates2[:], in_=gate2.rearrange("d p r -> p d r"))
 
         picked = {}
         words = [psum.tile([P, 2, P], F32, name="words%d" % b, tag="acc") for b in range(TURNED)]

@@ -21,7 +21,6 @@ PACK = 4
 BANK = 512
 LIST = 16
 TURNED = 3
-GROUPS = ((0, 1), (2,), (3,))
 
 
 def load_scale_rows(queue, tile, rows):
@@ -49,21 +48,19 @@ def tile_picked_hop2_gelu_p_kernel(
         offs_t = lists.tile([P, S // LIST], U16, name="offs_t")
         nc.sync.dma_start(offs_t[:], offs)
         w1_rows = w1.rearrange("(p j) c -> p j c", j=PACK)
-        cuts = (0, 128, 384, 512)
-        w1_raw = [
-            keep.tile([P, PACK, cuts[i + 1] - cuts[i]], F32, name="w1_raw%d" % i, tag="w1_raw%d" % i) for i in range(3)
-        ]
-        nc.sync.dma_start(out=w1_raw[0][:], in_=w1_rows[:, :, cuts[0] : cuts[1]])
+        cuts = (0, 1, 3, 4)
+        w1_raw = keep.tile([P, PACK, H], F32, name="w1_raw", tag="w1_raw0")
+        nc.sync.dma_start(out=w1_raw[:, cuts[0] : cuts[1], :], in_=w1_rows[:, cuts[0] : cuts[1], :])
         small = []
         for name, src, n in (("pos1", pos1, V), ("pos2", pos2, V), ("nxt1", nxt1, U), ("nxt2", nxt2, U)):
             t_ = lists.tile([P, n // LIST], U16, name=name + "_t")
             nc.sync.dma_start(t_[:], src)
             small.append(t_)
-        nc.sync.dma_start(out=xs[:].bitcast(I32)[0:P:8, :], in_=x_scales[0].bitcast(I32))
+        nc.sync.dma_start(out=xs[:].bitcast(I32)[32:96:4, :], in_=x_scales[0].bitcast(I32))
         xw = keep.tile([P, T], I32, name="xw", tag="xw", align_bytes=64)
         nc.sync.dma_start(out=xw[:], in_=x_words[0].rearrange("p n t -> p (n t)").bitcast(I32))
         for i in (1, 2):
-            nc.sync.dma_start(out=w1_raw[i][:], in_=w1_rows[:, :, cuts[i] : cuts[i + 1]])
+            nc.sync.dma_start(out=w1_raw[:, cuts[i] : cuts[i + 1], :], in_=w1_rows[:, cuts[i] : cuts[i + 1], :])
 
         warm = keep.tile([P, 1], F32, name="warm")
         nc.scalar.activation(warm[:], ident[:, 0:1], ACT.Gelu_apprx_tanh)
@@ -71,7 +68,7 @@ def tile_picked_hop2_gelu_p_kernel(
         gs_raw = keep.tile([P, S], U8, name="gs_raw", tag="gs_raw", align_bytes=64)
         nc.vector.tensor_copy(gs_raw[:], xs[:].indirect(offs_t[:]))
         for r in range(4):
-            nc.scalar.dma_start(out=gs[:].bitcast(I32)[r:P:32, :], in_=gs_raw[:].bitcast(I32)[8 * r : P : 32, :])
+            nc.sync.dma_start(out=gs[:].bitcast(I32)[r:P:32, :], in_=gs_raw[:].bitcast(I32)[32 + 4 * r : 96 : 16, :])
         gate_t = keep.tile([P, 2, V], F32, name="gate_t", tag="xs", align_bytes=64)
         nc.sync.dma_start(out=gate_t[:], in_=gate.rearrange("d p v -> p d v"))
         gates = [gate_t[:, d, :] for d in range(2)]
@@ -87,32 +84,37 @@ def tile_picked_hop2_gelu_p_kernel(
         nc.vector.memset(w2s[:].bitcast(I32), 0)
         load_scale_rows(nc.sync, w2s, w2_scales[0])
 
-        first = keep.tile([P, P * PACK], BF16, name="first", tag="grouped", align_bytes=64)
-        for i in range(3):
-            nc.scalar.copy(
-                first[:].rearrange("p (m j) -> p m j", j=PACK)[:, cuts[i] // 4 : cuts[i + 1] // 4],
-                w1_raw[i][:].rearrange("p j (m t) -> p m j t", t=PACK)[:, :, :, 0],
-            )
+        planes = w1_raw[:].rearrange("p j (m t) -> p m j t", t=PACK)
 
+        def quantise_w1(source, name, count):
+            codes = keep.tile([P, count * P], U32, name="w1c" + name, align_bytes=64)
+            scales = keep.tile([P, count * P], U8, name="w1s" + name, align_bytes=64)
+            nc.vector.quantize_mx(out=codes[:].bitcast(FP8X4), scales=scales[:], in_=source)
+            return [(codes[:, e * P : (e + 1) * P], scales[:, e * P : (e + 1) * P]) for e in range(count)]
+
+        def deal(tile, t, j0, j1):
+            nc.scalar.copy(tile[:].rearrange("p (m j) -> p m j", j=PACK)[:, :, j0:j1], planes[:, :, j0:j1, t])
+
+        first = keep.tile([P, P * PACK], BF16, name="first", tag="grouped", align_bytes=64)
+        second = keep.tile([P, P * PACK], BF16, name="second", align_bytes=64)
+        for i in range(3):
+            deal(first, 0, cuts[i], cuts[i + 1])
+        deal(second, 1, cuts[0], cuts[1])
+        deal(second, 1, cuts[1], cuts[3])
+        w1q = quantise_w1(first[:], "0", 1) + quantise_w1(second[:], "1", 1)
+        high = keep.tile([P, 2 * P * PACK], BF16, name="high", tag="grouped", align_bytes=64)
+        nc.vector.tensor_copy(high[:].rearrange("p (t m j) -> p m j t", t=2, j=PACK), planes[:, :, :, 2:])
+        w1q = w1q + quantise_w1(high[:], "23", 2)
         h = []
         for t in range(PACK):
-            if t == 1:
-                rest = keep.tile([P, 3 * P * PACK], BF16, name="rest", tag="grouped", align_bytes=64)
-                for i in range(3):
-                    nc.vector.tensor_copy(
-                        rest[:].rearrange("p (t m j) -> p m j t", t=3, j=PACK)[:, cuts[i] // 4 : cuts[i + 1] // 4],
-                        w1_raw[i][:].rearrange("p j (m t) -> p m j t", t=PACK)[:, :, :, 1:],
-                    )
-            w1c = keep.tile([P, P], U32, name="w1c%d" % t, align_bytes=64)
-            w1s = keep.tile([P, P], U8, name="w1s%d" % t, align_bytes=64)
-            source = first[:] if t == 0 else rest[:, (t - 1) * 512 : t * 512]
-            nc.vector.quantize_mx(out=w1c[:].bitcast(FP8X4), scales=w1s[:], in_=source)
+            w1c, w1s = w1q[t]
             ht = keep.tile([P, S], F32, name="h%d" % t)
-            width = 256 if t == 0 else BANK
-            for start in range(0, S, width):
+            edges = (0, 256, 512, 768, 1024) if t == 0 else (0, BANK, S)
+            for start, end in zip(edges[:-1], edges[1:]):
+                width = end - start
                 acc = psum.tile([P, width], F32, name="acc", tag="acc")
                 nc.tensor.matmul_mx(
-                    out=acc[:], lhsT=w1c[:].bitcast(FP8X4), lhsT_scale=w1s[:],
+                    out=acc[:], lhsT=w1c.bitcast(FP8X4), lhsT_scale=w1s,
                     rhs=gw[start // BANK][:, start % BANK : start % BANK + width].bitcast(FP8X4),
                     rhs_scale=gs[:, start : start + width],
                     start=True, stop=True,

@@ -20,6 +20,7 @@ P = 128
 PACK = 4
 BANK = 512
 LIST = 16
+X_AHEAD = 1280
 TURNED = 3
 
 
@@ -37,7 +38,9 @@ def tile_picked_hop2_gelu_p_kernel(
         keep = ctx.enter_context(tc.tile_pool(name="keep", bufs=1))
         psum = ctx.enter_context(tc.psum_pool(name="psum", bufs=4))
 
-        xs = keep.tile([P, T], U8, name="xs", tag="xs", align_bytes=64)
+        over = ctx.enter_context(tc.tile_pool(name="over", bufs=1))
+
+        xs = over.tile([P, T], U8, name="xs", offset=0, align_bytes=64)
         nc.vector.memset(xs[:].bitcast(I32), 0)
         ident = keep.tile([P, P], F32, name="ident")
         nc.vector.memset(ident[:], 0.0)
@@ -45,22 +48,19 @@ def tile_picked_hop2_gelu_p_kernel(
         gs = keep.tile([P, S], U8, name="gs", align_bytes=64)
         nc.vector.memset(gs[:].bitcast(I32), 0)
 
+        x_rows = x_words[0].rearrange("p n t -> p (n t)").bitcast(I32)
+        xw = keep.tile([P, T], I32, name="xw", align_bytes=64)
+        nc.sync.dma_start(out=xw[:, :X_AHEAD], in_=x_rows[:, :X_AHEAD])
         offs_t = lists.tile([P, S // LIST], U16, name="offs_t")
         nc.sync.dma_start(offs_t[:], offs)
-        w1_rows = w1.rearrange("(p j) c -> p j c", j=PACK)
-        cuts = (0, 1, 3, 4)
-        w1_raw = keep.tile([P, PACK, H], F32, name="w1_raw", tag="w1_raw0")
-        nc.sync.dma_start(out=w1_raw[:, cuts[0] : cuts[1], :], in_=w1_rows[:, cuts[0] : cuts[1], :])
-        small = []
-        for name, src, n in (("pos1", pos1, V), ("pos2", pos2, V), ("nxt1", nxt1, U), ("nxt2", nxt2, U)):
-            t_ = lists.tile([P, n // LIST], U16, name=name + "_t")
-            nc.sync.dma_start(t_[:], src)
-            small.append(t_)
         nc.sync.dma_start(out=xs[:].bitcast(I32)[32:96:4, :], in_=x_scales[0].bitcast(I32))
-        xw = keep.tile([P, T], I32, name="xw", tag="xw", align_bytes=64)
-        nc.sync.dma_start(out=xw[:], in_=x_words[0].rearrange("p n t -> p (n t)").bitcast(I32))
-        for i in (1, 2):
-            nc.sync.dma_start(out=w1_raw[:, cuts[i] : cuts[i + 1], :], in_=w1_rows[:, cuts[i] : cuts[i + 1], :])
+        nc.sync.dma_start(out=xw[:, X_AHEAD:], in_=x_rows[:, X_AHEAD:])
+        w1_rows = w1.rearrange("(p j) c -> p j c", j=PACK)
+        w1_raw = []
+        for i in range(2):
+            raw = keep.tile([P, 2, H], F32, name="w1_raw%d" % i)
+            nc.sync.dma_start(out=raw[:], in_=w1_rows[:, 2 * i : 2 * i + 2, :])
+            w1_raw.append(raw)
 
         warm = keep.tile([P, 1], F32, name="warm")
         nc.scalar.activation(warm[:], ident[:, 0:1], ACT.Gelu_apprx_tanh)
@@ -69,9 +69,23 @@ def tile_picked_hop2_gelu_p_kernel(
         nc.vector.tensor_copy(gs_raw[:], xs[:].indirect(offs_t[:]))
         for r in range(4):
             nc.sync.dma_start(out=gs[:].bitcast(I32)[r:P:32, :], in_=gs_raw[:].bitcast(I32)[32 + 4 * r : 96 : 16, :])
-        gate_t = keep.tile([P, 2, V], F32, name="gate_t", tag="xs", align_bytes=64)
+        small = []
+
+        def load_list(name, src, n):
+            t_ = lists.tile([P, n // LIST], U16, name=name + "_t")
+            nc.sync.dma_start(t_[:], src)
+            small.append(t_)
+
+        load_list("pos1", pos1, V)
+        load_list("pos2", pos2, V)
+        gate_t = over.tile([P, 2, V], F32, name="gate_t", offset=N, align_bytes=64)
         nc.sync.dma_start(out=gate_t[:], in_=gate.rearrange("d p v -> p d v"))
         gates = [gate_t[:, d, :] for d in range(2)]
+        load_list("nxt1", nxt1, U)
+        load_list("nxt2", nxt2, U)
+        w2s = over.tile([P, N], U8, name="w2s", offset=0, align_bytes=64)
+        nc.vector.memset(w2s[:].bitcast(I32), 0)
+        load_scale_rows(nc.sync, w2s, w2_scales[0])
         w2w = keep.tile([P, N], I32, name="w2w", tag="gs_raw", align_bytes=64)
         nc.sync.dma_start(out=w2w[:], in_=w2_words[0].rearrange("p n t -> p (n t)").bitcast(I32))
         gw = []
@@ -80,35 +94,33 @@ def tile_picked_hop2_gelu_p_kernel(
             nc.vector.tensor_copy(g_[:], xw[:].bitcast(U32).indirect(offs_t[:, half * 32 : (half + 1) * 32]))
             gw.append(g_)
 
-        w2s = keep.tile([P, N], U8, name="w2s", tag="xw", align_bytes=64)
-        nc.vector.memset(w2s[:].bitcast(I32), 0)
-        load_scale_rows(nc.sync, w2s, w2_scales[0])
-
-        planes = w1_raw[:].rearrange("p j (m t) -> p m j t", t=PACK)
-
         def quantise_w1(source, name, count):
             codes = keep.tile([P, count * P], U32, name="w1c" + name, align_bytes=64)
             scales = keep.tile([P, count * P], U8, name="w1s" + name, align_bytes=64)
             nc.vector.quantize_mx(out=codes[:].bitcast(FP8X4), scales=scales[:], in_=source)
             return [(codes[:, e * P : (e + 1) * P], scales[:, e * P : (e + 1) * P]) for e in range(count)]
 
-        def deal(tile, t, j0, j1):
-            nc.scalar.copy(tile[:].rearrange("p (m j) -> p m j", j=PACK)[:, :, j0:j1], planes[:, :, j0:j1, t])
+        def deal(copy, i, t0, t1, m0=0, m1=P):
+            copy(
+                dealt[t0 // 2][:].rearrange("p (t m j) -> p m j t", t=2, j=PACK)[
+                    :, m0:m1, 2 * i : 2 * i + 2, t0 % 2 : t0 % 2 + t1 - t0
+                ],
+                w1_raw[i][:].rearrange("p j (m t) -> p m j t", t=PACK)[:, m0:m1, :, t0:t1],
+            )
 
-        first = keep.tile([P, P * PACK], BF16, name="first", tag="grouped", align_bytes=64)
-        second = keep.tile([P, P * PACK], BF16, name="second", align_bytes=64)
-        for i in range(3):
-            deal(first, 0, cuts[i], cuts[i + 1])
-        deal(second, 1, cuts[0], cuts[1])
-        deal(second, 1, cuts[1], cuts[3])
-        w1q = quantise_w1(first[:], "0", 1) + quantise_w1(second[:], "1", 1)
-        high = keep.tile([P, 2 * P * PACK], BF16, name="high", tag="grouped", align_bytes=64)
-        nc.vector.tensor_copy(high[:].rearrange("p (t m j) -> p m j t", t=2, j=PACK), planes[:, :, :, 2:])
-        w1q = w1q + quantise_w1(high[:], "23", 2)
+        dealt = [keep.tile([P, 2 * P * PACK], BF16, name="dealt%d" % u, align_bytes=64) for u in range(2)]
+        deal(nc.scalar.copy, 0, 0, 2)
+        deal(nc.scalar.copy, 0, 2, 4)
+        deal(nc.scalar.copy, 1, 0, 1, 0, P // 2)
+        deal(nc.vector.tensor_copy, 1, 0, 2, P // 2, P)
+        deal(nc.scalar.copy, 1, 1, 2, 0, P // 2)
+        deal(nc.vector.tensor_copy, 1, 2, 4)
+        w1q = quantise_w1(dealt[0][:, : P * PACK], "0", 1) + quantise_w1(dealt[0][:, P * PACK :], "1", 1)
+        w1q = w1q + quantise_w1(dealt[1][:], "23", 2)
         h = []
         for t in range(PACK):
             w1c, w1s = w1q[t]
-            ht = keep.tile([P, S], F32, name="h%d" % t)
+            ht = keep.tile([P, S], F32, name="h%d" % t, align_bytes=64)
             edges = (0, 256, 512, 768, 1024) if t == 0 else (0, BANK, S)
             for start, end in zip(edges[:-1], edges[1:]):
                 width = end - start
@@ -122,11 +134,13 @@ def tile_picked_hop2_gelu_p_kernel(
                 nc.scalar.activation(ht[:, start : start + width], acc[:], ACT.Gelu_apprx_tanh)
             h.append(ht)
 
-        gates2 = keep.tile([P, 2, U], F32, name="gates2", tag="w1_raw0")
+        gates2 = keep.tile([P, 2, U], F32, name="gates2", tag="w1_raw1")
         nc.sync.dma_start(out=gates2[:], in_=gate2.rearrange("d p r -> p d r"))
 
         picked = {}
-        words = [psum.tile([P, 2, P], F32, name="words%d" % b, tag="acc") for b in range(TURNED)]
+        words01 = psum.tile([P, 2, 2, P], F32, name="words01", tag="acc")
+        words2 = psum.tile([P, 2, P], F32, name="words2", tag="acc")
+        words = [words01[:, 0], words01[:, 1], words2[:]]
         for u in range(2):
             for t in (2 * u, 2 * u + 1):
                 if t < PACK - 1:
@@ -160,23 +174,27 @@ def tile_picked_hop2_gelu_p_kernel(
 
         zb01 = keep.tile([P, 2 * P * PACK], BF16, name="zb01", tag="zb01", align_bytes=64)
         zb2 = keep.tile([P, P * PACK], BF16, name="zb2", align_bytes=64)
-        for b in range(TURNED):
-            target = zb01[:, b * 512 : (b + 1) * 512] if b < 2 else zb2[:]
-            nc.scalar.copy(target.bitcast(F32).rearrange("p (v u) -> p v u", u=2), words[b][:].rearrange("p u v -> p v u"))
+        nc.scalar.copy(
+            zb01[:].bitcast(F32).rearrange("p (b v u) -> p b v u", b=2, u=2), words01[:].rearrange("p b u v -> p b v u")
+        )
+        nc.scalar.copy(zb2[:].bitcast(F32).rearrange("p (v u) -> p v u", u=2), words2[:].rearrange("p u v -> p v u"))
 
         terms = [keep.tile([P, PACK, P], F32, name="term%d" % d, tag="late%d0" % d) for d in range(2)]
-        for t in range(PACK):
-            for d in range(2):
+        for d in range(2):
+            for t in range(PACK):
                 nc.vector.tensor_tensor(
                     terms[d][:, t, :], h[t][:].indirect(small[d][:, TURNED * 8 :]), gates[d][:, TURNED * P :], ALU.mult
                 )
 
         g = keep.tile([P, V], F32, name="g")
 
-        def second_layer(zb, start, width):
-            zc = keep.tile([P, width], U32, name="zc%d" % start, align_bytes=64)
+        def second_layer(zb, start, width, tag):
+            zc = keep.tile([P, width], U32, name="zc%d" % start, tag=tag, align_bytes=64)
             zs = keep.tile([P, width], U8, name="zs%d" % start, align_bytes=64)
-            nc.vector.quantize_mx(out=zc[:].bitcast(FP8X4), scales=zs[:], in_=zb[:])
+            for c in range(0, width, P):
+                nc.vector.quantize_mx(
+                    out=zc[:, c : c + P].bitcast(FP8X4), scales=zs[:, c : c + P], in_=zb[:, PACK * c : PACK * (c + P)]
+                )
             acc2 = psum.tile([P, width], F32, name="acc2", tag="turned")
             nc.tensor.matmul_mx(
                 out=acc2[:], lhsT=w2w[:].bitcast(FP8X4), lhsT_scale=w2s[:],
@@ -184,16 +202,16 @@ def tile_picked_hop2_gelu_p_kernel(
             )
             nc.scalar.activation(g[:, start : start + width], acc2[:], ACT.Relu)
 
-        second_layer(zb01, 0, 256)
-        zb3 = keep.tile([P, P * PACK], BF16, name="zb3", tag="zb01", align_bytes=64)
+        second_layer(zb01[:], 0, 256, "h2")
+        zb3 = zb01[:, : P * PACK]
         nc.vector.tensor_tensor(
-            zb3[:].rearrange("p (c i t) -> p c t i", i=4, t=PACK),
+            zb3.rearrange("p (c i t) -> p c t i", i=4, t=PACK),
             terms[0][:].rearrange("p t (c i) -> p c t i", i=4),
             terms[1][:].rearrange("p t (c i) -> p c t i", i=4),
             ALU.add,
         )
-        second_layer(zb2, 256, 128)
-        second_layer(zb3, 384, 128)
+        second_layer(zb2[:], 256, 128, "zc2")
+        second_layer(zb3, 384, 128, "zc3")
 
         half = U // 2
         o = [[keep.tile([P, half], F32, name="o%d%d" % (d, i)) for d in range(2)] for i in range(2)]

@@ -21,6 +21,7 @@ PACK = 4
 BANK = 512
 LIST = 16
 X_AHEAD = 1280
+SHARE = 88
 TURNED = 3
 
 
@@ -56,11 +57,8 @@ def tile_picked_hop2_gelu_p_kernel(
         nc.sync.dma_start(out=xs[:].bitcast(I32)[32:96:4, :], in_=x_scales[0].bitcast(I32))
         nc.sync.dma_start(out=xw[:, X_AHEAD:], in_=x_rows[:, X_AHEAD:])
         w1_rows = w1.rearrange("(p j) c -> p j c", j=PACK)
-        w1_raw = []
-        for i in range(2):
-            raw = keep.tile([P, 2, H], F32, name="w1_raw%d" % i)
-            nc.sync.dma_start(out=raw[:], in_=w1_rows[:, 2 * i : 2 * i + 2, :])
-            w1_raw.append(raw)
+        w1_raw = keep.tile([P, PACK, H], F32, name="w1_raw")
+        nc.sync.dma_start(out=w1_raw[:], in_=w1_rows)
 
         warm = keep.tile([P, 1], F32, name="warm")
         nc.scalar.activation(warm[:], ident[:, 0:1], ACT.Gelu_apprx_tanh)
@@ -100,22 +98,19 @@ def tile_picked_hop2_gelu_p_kernel(
             nc.vector.quantize_mx(out=codes[:].bitcast(FP8X4), scales=scales[:], in_=source)
             return [(codes[:, e * P : (e + 1) * P], scales[:, e * P : (e + 1) * P]) for e in range(count)]
 
-        def deal(copy, i, t0, t1, m0=0, m1=P):
+        def deal(copy, u, m0, m1):
             copy(
-                dealt[t0 // 2][:].rearrange("p (t m j) -> p m j t", t=2, j=PACK)[
-                    :, m0:m1, 2 * i : 2 * i + 2, t0 % 2 : t0 % 2 + t1 - t0
-                ],
-                w1_raw[i][:].rearrange("p j (m t) -> p m j t", t=PACK)[:, m0:m1, :, t0:t1],
+                dealt[u][:].rearrange("p (t m j) -> p m j t", t=2, j=PACK)[:, m0:m1],
+                w1_raw[:].rearrange("p j (m t) -> p m j t", t=PACK)[:, m0:m1, :, 2 * u : 2 * u + 2],
             )
 
         dealt = [keep.tile([P, 2 * P * PACK], BF16, name="dealt%d" % u, align_bytes=64) for u in range(2)]
-        deal(nc.scalar.copy, 0, 0, 2)
-        deal(nc.scalar.copy, 0, 2, 4)
-        deal(nc.scalar.copy, 1, 0, 1, 0, P // 2)
-        deal(nc.vector.tensor_copy, 1, 0, 2, P // 2, P)
-        deal(nc.scalar.copy, 1, 1, 2, 0, P // 2)
-        deal(nc.vector.tensor_copy, 1, 2, 4)
+        for u in range(2):
+            deal(nc.scalar.copy, u, SHARE, P)
+        deal(nc.vector.tensor_copy, 0, 0, SHARE)
+        deal(nc.vector.tensor_copy, 1, 0, SHARE // 2)
         w1q = quantise_w1(dealt[0][:, : P * PACK], "0", 1) + quantise_w1(dealt[0][:, P * PACK :], "1", 1)
+        deal(nc.vector.tensor_copy, 1, SHARE // 2, SHARE)
         w1q = w1q + quantise_w1(dealt[1][:], "23", 2)
         h = []
         for t in range(PACK):
@@ -134,7 +129,7 @@ def tile_picked_hop2_gelu_p_kernel(
                 nc.scalar.activation(ht[:, start : start + width], acc[:], ACT.Gelu_apprx_tanh)
             h.append(ht)
 
-        gates2 = keep.tile([P, 2, U], F32, name="gates2", tag="w1_raw1")
+        gates2 = keep.tile([P, 2, U], F32, name="gates2", tag="w1_raw")
         nc.sync.dma_start(out=gates2[:], in_=gate2.rearrange("d p r -> p d r"))
 
         picked = {}

@@ -20,8 +20,9 @@ P = 128
 PACK = 4
 BANK = 512
 LIST = 16
-X_AHEAD = 1280
-SHARE = 88
+X_AHEAD = 1024
+SHARE = 96
+LATER_SHARE = 100
 TURNED = 3
 
 
@@ -49,6 +50,9 @@ def tile_picked_hop2_gelu_p_kernel(
         gs = keep.tile([P, S], U8, name="gs", align_bytes=64)
         nc.vector.memset(gs[:].bitcast(I32), 0)
 
+        w2s = keep.tile([P, N], U8, name="w2s", align_bytes=64)
+        nc.vector.memset(w2s[:].bitcast(I32), 0)
+
         x_rows = x_words[0].rearrange("p n t -> p (n t)").bitcast(I32)
         xw = keep.tile([P, T], I32, name="xw", align_bytes=64)
         nc.sync.dma_start(out=xw[:, :X_AHEAD], in_=x_rows[:, :X_AHEAD])
@@ -58,7 +62,7 @@ def tile_picked_hop2_gelu_p_kernel(
         nc.sync.dma_start(out=xw[:, X_AHEAD:], in_=x_rows[:, X_AHEAD:])
         w1_rows = w1.rearrange("(p j) c -> p j c", j=PACK)
         w1_raw = keep.tile([P, PACK, H], F32, name="w1_raw")
-        nc.sync.dma_start(out=w1_raw[:], in_=w1_rows)
+        nc.sync.dma_start(out=w1_raw[:, :3, :], in_=w1_rows[:, :3, :])
 
         warm = keep.tile([P, 1], F32, name="warm")
         nc.scalar.activation(warm[:], ident[:, 0:1], ACT.Gelu_apprx_tanh)
@@ -67,6 +71,7 @@ def tile_picked_hop2_gelu_p_kernel(
         nc.vector.tensor_copy(gs_raw[:], xs[:].indirect(offs_t[:]))
         for r in range(4):
             nc.sync.dma_start(out=gs[:].bitcast(I32)[r:P:32, :], in_=gs_raw[:].bitcast(I32)[32 + 4 * r : 96 : 16, :])
+        nc.sync.dma_start(out=w1_raw[:, 3:, :], in_=w1_rows[:, 3:, :])
         small = []
 
         def load_list(name, src, n):
@@ -81,8 +86,6 @@ def tile_picked_hop2_gelu_p_kernel(
         gates = [gate_t[:, d, :] for d in range(2)]
         load_list("nxt1", nxt1, U)
         load_list("nxt2", nxt2, U)
-        w2s = over.tile([P, N], U8, name="w2s", offset=0, align_bytes=64)
-        nc.vector.memset(w2s[:].bitcast(I32), 0)
         load_scale_rows(nc.sync, w2s, w2_scales[0])
         w2w = keep.tile([P, N], I32, name="w2w", tag="gs_raw", align_bytes=64)
         nc.sync.dma_start(out=w2w[:], in_=w2_words[0].rearrange("p n t -> p (n t)").bitcast(I32))
@@ -98,20 +101,21 @@ def tile_picked_hop2_gelu_p_kernel(
             nc.vector.quantize_mx(out=codes[:].bitcast(FP8X4), scales=scales[:], in_=source)
             return [(codes[:, e * P : (e + 1) * P], scales[:, e * P : (e + 1) * P]) for e in range(count)]
 
-        def deal(copy, u, m0, m1):
+        def deal(copy, dealt, columns, rows, planes):
             copy(
-                dealt[u][:].rearrange("p (t m j) -> p m j t", t=2, j=PACK)[:, m0:m1],
-                w1_raw[:].rearrange("p j (m t) -> p m j t", t=PACK)[:, m0:m1, :, 2 * u : 2 * u + 2],
+                dealt[:].rearrange("p (t m j) -> p m j t", m=P, j=PACK)[:, columns, rows, :],
+                w1_raw[:].rearrange("p j (m t) -> p m j t", t=PACK)[:, columns, rows, planes],
             )
 
-        dealt = [keep.tile([P, 2 * P * PACK], BF16, name="dealt%d" % u, align_bytes=64) for u in range(2)]
-        for u in range(2):
-            deal(nc.scalar.copy, u, SHARE, P)
-        deal(nc.vector.tensor_copy, 0, 0, SHARE)
-        deal(nc.vector.tensor_copy, 1, 0, SHARE // 2)
-        w1q = quantise_w1(dealt[0][:, : P * PACK], "0", 1) + quantise_w1(dealt[0][:, P * PACK :], "1", 1)
-        deal(nc.vector.tensor_copy, 1, SHARE // 2, SHARE)
-        w1q = w1q + quantise_w1(dealt[1][:], "23", 2)
+        dealt0 = keep.tile([P, P * PACK], BF16, name="dealt0", tag="dealt", align_bytes=64)
+        deal(nc.scalar.copy, dealt0, slice(0, P), slice(0, 2), slice(0, 1))
+        deal(nc.scalar.copy, dealt0, slice(SHARE, P), slice(2, PACK), slice(0, 1))
+        deal(nc.vector.tensor_copy, dealt0, slice(0, SHARE), slice(2, PACK), slice(0, 1))
+        w1q = quantise_w1(dealt0[:], "0", 1)
+        others = keep.tile([P, 3 * P * PACK], BF16, name="others", tag="dealt", align_bytes=64)
+        deal(nc.scalar.copy, others, slice(LATER_SHARE, P), slice(0, PACK), slice(1, PACK))
+        deal(nc.vector.tensor_copy, others, slice(0, LATER_SHARE), slice(0, PACK), slice(1, PACK))
+        w1q = w1q + quantise_w1(others[:, : P * PACK], "1", 1) + quantise_w1(others[:, P * PACK :], "23", 2)
         h = []
         for t in range(PACK):
             w1c, w1s = w1q[t]

@@ -20,7 +20,8 @@ P = 128
 PACK = 4
 BANK = 512
 LIST = 16
-X_AHEAD = 1024
+W1_AHEAD = 1280
+X_AHEAD = 896
 SHARE = 96
 LATER_SHARE = 100
 TURNED = 3
@@ -60,9 +61,9 @@ def tile_picked_hop2_gelu_p_kernel(
         nc.sync.dma_start(offs_t[:], offs)
         nc.sync.dma_start(out=xs[:].bitcast(I32)[32:96:4, :], in_=x_scales[0].bitcast(I32))
         nc.sync.dma_start(out=xw[:, X_AHEAD:], in_=x_rows[:, X_AHEAD:])
-        w1_rows = w1.rearrange("(p j) c -> p j c", j=PACK)
-        w1_raw = keep.tile([P, PACK, H], F32, name="w1_raw")
-        nc.sync.dma_start(out=w1_raw[:, :3, :], in_=w1_rows[:, :3, :])
+        w1_rows = w1.rearrange("(p j) c -> p (j c)", j=PACK)
+        w1_raw = keep.tile([P, PACK * H], F32, name="w1_raw")
+        nc.sync.dma_start(out=w1_raw[:, :W1_AHEAD], in_=w1_rows[:, :W1_AHEAD])
 
         warm = keep.tile([P, 1], F32, name="warm")
         nc.scalar.activation(warm[:], ident[:, 0:1], ACT.Gelu_apprx_tanh)
@@ -71,7 +72,7 @@ def tile_picked_hop2_gelu_p_kernel(
         nc.vector.tensor_copy(gs_raw[:], xs[:].indirect(offs_t[:]))
         for r in range(4):
             nc.sync.dma_start(out=gs[:].bitcast(I32)[r:P:32, :], in_=gs_raw[:].bitcast(I32)[32 + 4 * r : 96 : 16, :])
-        nc.sync.dma_start(out=w1_raw[:, 3:, :], in_=w1_rows[:, 3:, :])
+        nc.sync.dma_start(out=w1_raw[:, W1_AHEAD:], in_=w1_rows[:, W1_AHEAD:])
         small = []
 
         def load_list(name, src, n):
@@ -104,7 +105,7 @@ def tile_picked_hop2_gelu_p_kernel(
         def deal(copy, dealt, columns, rows, planes):
             copy(
                 dealt[:].rearrange("p (t m j) -> p m j t", m=P, j=PACK)[:, columns, rows, :],
-                w1_raw[:].rearrange("p j (m t) -> p m j t", t=PACK)[:, columns, rows, planes],
+                w1_raw[:].rearrange("p (j m t) -> p m j t", j=PACK, t=PACK)[:, columns, rows, planes],
             )
 
         dealt0 = keep.tile([P, P * PACK], BF16, name="dealt0", tag="dealt", align_bytes=64)

@@ -20,16 +20,12 @@ P = 128
 PACK = 4
 BANK = 512
 LIST = 16
-W1_AHEAD = 1280
-X_AHEAD = 896
-SHARE = 96
-LATER_SHARE = 100
+BLOCK = P // LIST
 TURNED = 3
-
-
-def load_scale_rows(queue, tile, rows):
-    for r in range(4):
-        queue.dma_start(out=tile[:].bitcast(I32)[r:P:32, :], in_=rows.bitcast(I32)[r:16:4, :])
+X_AHEAD = 1024
+W1_AHEAD = 1408
+FIRST_SHARE = 96
+LATER_SHARE = 100
 
 
 def tile_picked_hop2_gelu_p_kernel(
@@ -40,7 +36,6 @@ def tile_picked_hop2_gelu_p_kernel(
         lists = ctx.enter_context(tc.tile_pool(name="lists", bufs=1))
         keep = ctx.enter_context(tc.tile_pool(name="keep", bufs=1))
         psum = ctx.enter_context(tc.psum_pool(name="psum", bufs=4))
-
         over = ctx.enter_context(tc.tile_pool(name="over", bufs=1))
 
         xs = over.tile([P, T], U8, name="xs", offset=0, align_bytes=64)
@@ -50,15 +45,18 @@ def tile_picked_hop2_gelu_p_kernel(
         make_identity(nc, ident[:], nomemset=True)
         gs = keep.tile([P, S], U8, name="gs", align_bytes=64)
         nc.vector.memset(gs[:].bitcast(I32), 0)
-
         w2s = keep.tile([P, N], U8, name="w2s", align_bytes=64)
         nc.vector.memset(w2s[:].bitcast(I32), 0)
+
+        def load_list(name, src, entries):
+            list_tile = lists.tile([P, entries // LIST], U16, name=name)
+            nc.sync.dma_start(list_tile[:], src)
+            return list_tile
 
         x_rows = x_words[0].rearrange("p n t -> p (n t)").bitcast(I32)
         xw = keep.tile([P, T], I32, name="xw", align_bytes=64)
         nc.sync.dma_start(out=xw[:, :X_AHEAD], in_=x_rows[:, :X_AHEAD])
-        offs_t = lists.tile([P, S // LIST], U16, name="offs_t")
-        nc.sync.dma_start(offs_t[:], offs)
+        offs_t = load_list("offs_t", offs, S)
         nc.sync.dma_start(out=xs[:].bitcast(I32)[32:96:4, :], in_=x_scales[0].bitcast(I32))
         nc.sync.dma_start(out=xw[:, X_AHEAD:], in_=x_rows[:, X_AHEAD:])
         w1_rows = w1.rearrange("(p j) c -> p (j c)", j=PACK)
@@ -70,37 +68,25 @@ def tile_picked_hop2_gelu_p_kernel(
 
         gs_raw = keep.tile([P, S], U8, name="gs_raw", tag="gs_raw", align_bytes=64)
         nc.vector.tensor_copy(gs_raw[:], xs[:].indirect(offs_t[:]))
-        for r in range(4):
+        for r in range(PACK):
             nc.sync.dma_start(out=gs[:].bitcast(I32)[r:P:32, :], in_=gs_raw[:].bitcast(I32)[32 + 4 * r : 96 : 16, :])
         nc.sync.dma_start(out=w1_raw[:, W1_AHEAD:], in_=w1_rows[:, W1_AHEAD:])
-        small = []
 
-        def load_list(name, src, n):
-            t_ = lists.tile([P, n // LIST], U16, name=name + "_t")
-            nc.sync.dma_start(t_[:], src)
-            small.append(t_)
-
-        load_list("pos1", pos1, V)
-        load_list("pos2", pos2, V)
+        pos = [load_list("pos1_t", pos1, V), load_list("pos2_t", pos2, V)]
         gate_t = over.tile([P, 2, V], F32, name="gate_t", offset=N, align_bytes=64)
         nc.sync.dma_start(out=gate_t[:], in_=gate.rearrange("d p v -> p d v"))
-        gates = [gate_t[:, d, :] for d in range(2)]
-        load_list("nxt1", nxt1, U)
-        load_list("nxt2", nxt2, U)
-        load_scale_rows(nc.sync, w2s, w2_scales[0])
+        nxt = [load_list("nxt1_t", nxt1, U), load_list("nxt2_t", nxt2, U)]
+        for r in range(PACK):
+            nc.sync.dma_start(out=w2s[:].bitcast(I32)[r:P:32, :], in_=w2_scales[0].bitcast(I32)[r:16:PACK, :])
         w2w = keep.tile([P, N], I32, name="w2w", tag="gs_raw", align_bytes=64)
         nc.sync.dma_start(out=w2w[:], in_=w2_words[0].rearrange("p n t -> p (n t)").bitcast(I32))
+
         gw = []
         for half in range(2):
-            g_ = keep.tile([P, BANK], U32, name="gw%d" % half, align_bytes=64)
-            nc.vector.tensor_copy(g_[:], xw[:].bitcast(U32).indirect(offs_t[:, half * 32 : (half + 1) * 32]))
-            gw.append(g_)
-
-        def quantise_w1(source, name, count):
-            codes = keep.tile([P, count * P], U32, name="w1c" + name, align_bytes=64)
-            scales = keep.tile([P, count * P], U8, name="w1s" + name, align_bytes=64)
-            nc.vector.quantize_mx(out=codes[:].bitcast(FP8X4), scales=scales[:], in_=source)
-            return [(codes[:, e * P : (e + 1) * P], scales[:, e * P : (e + 1) * P]) for e in range(count)]
+            gw_half = keep.tile([P, BANK], U32, name="gw%d" % half, align_bytes=64)
+            entries = offs_t[:, half * BANK // LIST : (half + 1) * BANK // LIST]
+            nc.vector.tensor_copy(gw_half[:], xw[:].bitcast(U32).indirect(entries))
+            gw.append(gw_half)
 
         def deal(copy, dealt, columns, rows, planes):
             copy(
@@ -108,22 +94,28 @@ def tile_picked_hop2_gelu_p_kernel(
                 w1_raw[:].rearrange("p (j m t) -> p m j t", j=PACK, t=PACK)[:, columns, rows, planes],
             )
 
+        def quantise_w1(source, name, count):
+            codes = keep.tile([P, count * P], U32, name="w1c" + name, align_bytes=64)
+            scales = keep.tile([P, count * P], U8, name="w1s" + name, align_bytes=64)
+            nc.vector.quantize_mx(out=codes[:].bitcast(FP8X4), scales=scales[:], in_=source)
+            return [(codes[:, e * P : (e + 1) * P], scales[:, e * P : (e + 1) * P]) for e in range(count)]
+
         dealt0 = keep.tile([P, P * PACK], BF16, name="dealt0", tag="dealt", align_bytes=64)
         deal(nc.scalar.copy, dealt0, slice(0, P), slice(0, 2), slice(0, 1))
-        deal(nc.scalar.copy, dealt0, slice(SHARE, P), slice(2, PACK), slice(0, 1))
-        deal(nc.vector.tensor_copy, dealt0, slice(0, SHARE), slice(2, PACK), slice(0, 1))
+        deal(nc.scalar.copy, dealt0, slice(FIRST_SHARE, P), slice(2, PACK), slice(0, 1))
+        deal(nc.vector.tensor_copy, dealt0, slice(0, FIRST_SHARE), slice(2, PACK), slice(0, 1))
         w1q = quantise_w1(dealt0[:], "0", 1)
         others = keep.tile([P, 3 * P * PACK], BF16, name="others", tag="dealt", align_bytes=64)
         deal(nc.scalar.copy, others, slice(LATER_SHARE, P), slice(0, PACK), slice(1, PACK))
         deal(nc.vector.tensor_copy, others, slice(0, LATER_SHARE), slice(0, PACK), slice(1, PACK))
         w1q = w1q + quantise_w1(others[:, : P * PACK], "1", 1) + quantise_w1(others[:, P * PACK :], "23", 2)
+
         h = []
         for t in range(PACK):
             w1c, w1s = w1q[t]
-            ht = keep.tile([P, S], F32, name="h%d" % t, align_bytes=64)
-            edges = (0, 256, 512, 768, 1024) if t == 0 else (0, BANK, S)
-            for start, end in zip(edges[:-1], edges[1:]):
-                width = end - start
+            h_t = keep.tile([P, S], F32, name="h%d" % t, align_bytes=64)
+            width = BANK // 2 if t == 0 else BANK
+            for start in range(0, S, width):
                 acc = psum.tile([P, width], F32, name="acc", tag="acc")
                 nc.tensor.matmul_mx(
                     out=acc[:], lhsT=w1c.bitcast(FP8X4), lhsT_scale=w1s,
@@ -131,35 +123,36 @@ def tile_picked_hop2_gelu_p_kernel(
                     rhs_scale=gs[:, start : start + width],
                     start=True, stop=True,
                 )
-                nc.scalar.activation(ht[:, start : start + width], acc[:], ACT.Gelu_apprx_tanh)
-            h.append(ht)
+                nc.scalar.activation(h_t[:, start : start + width], acc[:], ACT.Gelu_apprx_tanh)
+            h.append(h_t)
 
-        gates2 = keep.tile([P, 2, U], F32, name="gates2", tag="w1_raw")
-        nc.sync.dma_start(out=gates2[:], in_=gate2.rearrange("d p r -> p d r"))
+        gate2_t = keep.tile([P, 2, U], F32, name="gate2_t", tag="w1_raw")
+        nc.sync.dma_start(out=gate2_t[:], in_=gate2.rearrange("d p r -> p d r"))
+
+        def gather_term(term, t, d, first, last):
+            nc.vector.tensor_tensor(
+                term, h[t][:].indirect(pos[d][:, first * BLOCK : last * BLOCK]),
+                gate_t[:, d, first * P : last * P], ALU.mult,
+            )
 
         picked = {}
-        words01 = psum.tile([P, 2, 2, P], F32, name="words01", tag="acc")
-        words2 = psum.tile([P, 2, P], F32, name="words2", tag="acc")
-        words = [words01[:, 0], words01[:, 1], words2[:]]
+        back01 = psum.tile([P, 2, 2, P], F32, name="back01", tag="acc")
+        back2 = psum.tile([P, 2, P], F32, name="back2", tag="acc")
+        back = [back01[:, 0], back01[:, 1], back2[:]]
         for u in range(2):
             for t in (2 * u, 2 * u + 1):
                 if t < PACK - 1:
                     for d in range(2):
-                        pk = keep.tile([P, TURNED * P], F32, name="pk%d%d" % (t, d))
-                        nc.vector.tensor_tensor(
-                            pk[:], h[t][:].indirect(small[d][:, 0 : TURNED * 8]), gates[d][:, 0 : TURNED * P], ALU.mult
-                        )
+                        term = keep.tile([P, TURNED * P], F32, name="term%d%d" % (t, d))
+                        gather_term(term[:], t, d, 0, TURNED)
                         for b in range(TURNED):
-                            picked[t, d, b] = pk[:, b * P : (b + 1) * P]
+                            picked[t, d, b] = term[:, b * P : (b + 1) * P]
                 else:
                     for b in range(TURNED):
                         for d in range(2):
-                            pk = keep.tile([P, P], F32, name="pk%d%d%d" % (t, d, b), tag="late%d%d" % (d, b))
-                            nc.vector.tensor_tensor(
-                                pk[:], h[t][:].indirect(small[d][:, b * 8 : (b + 1) * 8]),
-                                gates[d][:, b * P : (b + 1) * P], ALU.mult,
-                            )
-                            picked[t, d, b] = pk[:]
+                            term = keep.tile([P, P], F32, name="term%d%d%d" % (t, d, b), tag="late%d%d" % (d, b))
+                            gather_term(term[:], t, d, b, b + 1)
+                            picked[t, d, b] = term[:]
             for b in range(TURNED):
                 turned = psum.tile([P, 2, P], F32, name="turned", tag="turned")
                 for e in range(2):
@@ -170,21 +163,19 @@ def tile_picked_hop2_gelu_p_kernel(
                         )
                 pairs = keep.tile([P, 2 * P], BF16, name="pairs%d%d" % (u, b), align_bytes=64)
                 nc.scalar.copy(pairs[:].rearrange("v (p e) -> v p e", e=2), turned[:].rearrange("v e p -> v p e"))
-                nc.tensor.transpose(words[b][:, u, :], pairs[:].bitcast(F32), ident[:])
+                nc.tensor.transpose(back[b][:, u, :], pairs[:].bitcast(F32), ident[:])
 
-        zb01 = keep.tile([P, 2 * P * PACK], BF16, name="zb01", tag="zb01", align_bytes=64)
+        zb01 = keep.tile([P, 2 * P * PACK], BF16, name="zb01", align_bytes=64)
         zb2 = keep.tile([P, P * PACK], BF16, name="zb2", align_bytes=64)
         nc.scalar.copy(
-            zb01[:].bitcast(F32).rearrange("p (b v u) -> p b v u", b=2, u=2), words01[:].rearrange("p b u v -> p b v u")
+            zb01[:].bitcast(F32).rearrange("p (b v u) -> p b v u", b=2, u=2), back01[:].rearrange("p b u v -> p b v u")
         )
-        nc.scalar.copy(zb2[:].bitcast(F32).rearrange("p (v u) -> p v u", u=2), words2[:].rearrange("p u v -> p v u"))
+        nc.scalar.copy(zb2[:].bitcast(F32).rearrange("p (v u) -> p v u", u=2), back2[:].rearrange("p u v -> p v u"))
 
-        terms = [keep.tile([P, PACK, P], F32, name="term%d" % d, tag="late%d0" % d) for d in range(2)]
+        direct = [keep.tile([P, PACK, P], F32, name="direct%d" % d, tag="late%d0" % d) for d in range(2)]
         for d in range(2):
             for t in range(PACK):
-                nc.vector.tensor_tensor(
-                    terms[d][:, t, :], h[t][:].indirect(small[d][:, TURNED * 8 :]), gates[d][:, TURNED * P :], ALU.mult
-                )
+                gather_term(direct[d][:, t, :], t, d, TURNED, TURNED + 1)
 
         g = keep.tile([P, V], F32, name="g")
 
@@ -192,8 +183,9 @@ def tile_picked_hop2_gelu_p_kernel(
             zc = keep.tile([P, width], U32, name="zc%d" % start, tag=tag, align_bytes=64)
             zs = keep.tile([P, width], U8, name="zs%d" % start, align_bytes=64)
             for c in range(0, width, P):
+                end = min(c + P, width)
                 nc.vector.quantize_mx(
-                    out=zc[:, c : c + P].bitcast(FP8X4), scales=zs[:, c : c + P], in_=zb[:, PACK * c : PACK * (c + P)]
+                    out=zc[:, c:end].bitcast(FP8X4), scales=zs[:, c:end], in_=zb[:, PACK * c : PACK * end]
                 )
             acc2 = psum.tile([P, width], F32, name="acc2", tag="turned")
             nc.tensor.matmul_mx(
@@ -202,26 +194,29 @@ def tile_picked_hop2_gelu_p_kernel(
             )
             nc.scalar.activation(g[:, start : start + width], acc2[:], ACT.Relu)
 
-        second_layer(zb01[:], 0, 256, "h2")
+        second_layer(zb01[:], 0, 2 * P, "h2")
         zb3 = zb01[:, : P * PACK]
-        nc.vector.tensor_tensor(
-            zb3.rearrange("p (c i t) -> p c t i", i=4, t=PACK),
-            terms[0][:].rearrange("p t (c i) -> p c t i", i=4),
-            terms[1][:].rearrange("p t (c i) -> p c t i", i=4),
-            ALU.add,
-        )
-        second_layer(zb2[:], 256, 128, "zc2")
-        second_layer(zb3, 384, 128, "zc3")
+        groups = P // 8
+        for i in range(2):
+            nc.vector.tensor_tensor(
+                zb3.rearrange("p (c i t) -> p c t i", i=4, t=PACK)[:, groups * i : groups * (i + 1)],
+                direct[0][:].rearrange("p t (c i) -> p c t i", i=4)[:, groups * i : groups * (i + 1)],
+                direct[1][:].rearrange("p t (c i) -> p c t i", i=4)[:, groups * i : groups * (i + 1)],
+                ALU.add,
+            )
+        second_layer(zb2[:], 2 * P, P, "zc2")
+        for i in range(2):
+            second_layer(zb01[:, 2 * P * i : 2 * P * (i + 1)], TURNED * P + i * P // 2, P // 2, "zc3%d" % i)
 
-        half = U // 2
-        o = [[keep.tile([P, half], F32, name="o%d%d" % (d, i)) for d in range(2)] for i in range(2)]
+        out0 = keep.tile([P, U], F32, name="out0")
+        nc.vector.tensor_tensor(out0[:], g[:].indirect(nxt[0][:]), gate2_t[:, 0, :], ALU.mult)
+        out1 = [keep.tile([P, P], F32, name="out1%d" % i) for i in range(2)]
         for i in range(2):
-            for d in range(2):
-                nc.vector.tensor_tensor(
-                    o[i][d][:], g[:].indirect(small[2 + d][:, 8 * i : 8 * i + 8]),
-                    gates2[:, d, half * i : half * (i + 1)], ALU.mult,
-                )
+            nc.vector.tensor_tensor(
+                out1[i][:], g[:].indirect(nxt[1][:, BLOCK * i : BLOCK * (i + 1)]),
+                gate2_t[:, 1, P * i : P * (i + 1)], ALU.mult,
+            )
         for i in range(2):
-            res = keep.tile([P, half], F32, name="res%d" % i)
-            nc.vector.tensor_tensor(res[:], o[i][0][:], o[i][1][:], ALU.add)
-            nc.sync.dma_start(out=out[:, half * i : half * (i + 1)], in_=res[:])
+            res = keep.tile([P, P], F32, name="res%d" % i)
+            nc.vector.tensor_tensor(res[:], out0[:, P * i : P * (i + 1)], out1[i][:], ALU.add)
+            nc.sync.dma_start(out=out[:, P * i : P * (i + 1)], in_=res[:])

@@ -78,15 +78,22 @@ def tile_picked_hop2_gelu_p_kernel(
         nxt = [load_list("nxt1_t", nxt1, U), load_list("nxt2_t", nxt2, U)]
         for r in range(PACK):
             nc.sync.dma_start(out=w2s[:].bitcast(I32)[r:P:32, :], in_=w2_scales[0].bitcast(I32)[r:16:PACK, :])
-        w2w = keep.tile([P, N], I32, name="w2w", tag="gs_raw", align_bytes=64)
-        nc.sync.dma_start(out=w2w[:], in_=w2_words[0].rearrange("p n t -> p (n t)").bitcast(I32))
-
         gw = []
         for half in range(2):
             gw_half = keep.tile([P, BANK], U32, name="gw%d" % half, align_bytes=64)
             entries = offs_t[:, half * BANK // LIST : (half + 1) * BANK // LIST]
             nc.vector.tensor_copy(gw_half[:], xw[:].bitcast(U32).indirect(entries))
             gw.append(gw_half)
+
+        for i in range(2):
+            idle = psum.tile([P, BANK], F32, name="idle", tag="turned")
+            nc.tensor.matmul_mx(
+                out=idle[:], lhsT=gw[0][:, :P].bitcast(FP8X4), lhsT_scale=gs_raw[:, :P],
+                rhs=gw[0][:].bitcast(FP8X4), rhs_scale=gs_raw[:, :BANK], start=True, stop=True,
+            )
+
+        w2w = keep.tile([P, N], I32, name="w2w", tag="gs_raw", align_bytes=64)
+        nc.sync.dma_start(out=w2w[:], in_=w2_words[0].rearrange("p n t -> p (n t)").bitcast(I32))
 
         def deal(copy, dealt, columns, rows, planes):
             copy(

@@ -21,7 +21,8 @@ PACK = 4
 BANK = 512
 LIST = 16
 BLOCK = P // LIST
-TURNED = 3
+SPLIT = 2
+SHARED = 160
 X_AHEAD = 1024
 W1_AHEAD = 1408
 FIRST_SHARE = 96
@@ -35,7 +36,11 @@ def tile_picked_hop2_gelu_p_kernel(
     with ExitStack() as ctx:
         lists = ctx.enter_context(tc.tile_pool(name="lists", bufs=1))
         keep = ctx.enter_context(tc.tile_pool(name="keep", bufs=1))
-        psum = ctx.enter_context(tc.psum_pool(name="psum", bufs=4))
+        psum = ctx.enter_context(tc.psum_pool(name="psum", bufs=1))
+
+        def bank(name, number, shape):
+            return psum.tile(shape, F32, name=name, tag="bank%d" % number)
+
         over = ctx.enter_context(tc.tile_pool(name="over", bufs=1))
 
         xs = over.tile([P, T], U8, name="xs", offset=0, align_bytes=64)
@@ -75,6 +80,12 @@ def tile_picked_hop2_gelu_p_kernel(
         pos = [load_list("pos1_t", pos1, V), load_list("pos2_t", pos2, V)]
         gate_t = over.tile([P, 2, V], F32, name="gate_t", offset=N, align_bytes=64)
         nc.sync.dma_start(out=gate_t[:], in_=gate.rearrange("d p v -> p d v"))
+        gate_col = []
+        for d in range(2):
+            col = keep.tile([P, SPLIT], F32, name="gate_col%d" % d)
+            with nc.allow_non_contiguous_dma(reason="one gate value a partition"):
+                nc.sync.dma_start(out=col[:], in_=gate[d, 0, : SPLIT * P].rearrange("(b v) -> v b", v=P))
+            gate_col.append(col)
         nxt = [load_list("nxt1_t", nxt1, U), load_list("nxt2_t", nxt2, U)]
         for r in range(PACK):
             nc.sync.dma_start(out=w2s[:].bitcast(I32)[r:P:32, :], in_=w2_scales[0].bitcast(I32)[r:16:PACK, :])
@@ -86,7 +97,7 @@ def tile_picked_hop2_gelu_p_kernel(
             gw.append(gw_half)
 
         for i in range(2):
-            idle = psum.tile([P, BANK], F32, name="idle", tag="turned")
+            idle = bank("idle%d" % i, 4 + i, [P, BANK])
             nc.tensor.matmul_mx(
                 out=idle[:], lhsT=gw[0][:, :P].bitcast(FP8X4), lhsT_scale=gs_raw[:, :P],
                 rhs=gw[0][:].bitcast(FP8X4), rhs_scale=gs_raw[:, :BANK], start=True, stop=True,
@@ -118,12 +129,15 @@ def tile_picked_hop2_gelu_p_kernel(
         w1q = w1q + quantise_w1(others[:, : P * PACK], "1", 1) + quantise_w1(others[:, P * PACK :], "23", 2)
 
         h = []
-        for t in range(PACK):
+        products = []
+
+        def first_layer(t):
             w1c, w1s = w1q[t]
             h_t = keep.tile([P, S], F32, name="h%d" % t, align_bytes=64)
             width = BANK // 2 if t == 0 else BANK
             for start in range(0, S, width):
-                acc = psum.tile([P, width], F32, name="acc", tag="acc")
+                acc = bank("acc%d" % len(products), len(products) % 4, [P, width])
+                products.append(acc)
                 nc.tensor.matmul_mx(
                     out=acc[:], lhsT=w1c.bitcast(FP8X4), lhsT_scale=w1s,
                     rhs=gw[start // BANK][:, start % BANK : start % BANK + width].bitcast(FP8X4),
@@ -132,6 +146,9 @@ def tile_picked_hop2_gelu_p_kernel(
                 )
                 nc.scalar.activation(h_t[:, start : start + width], acc[:], ACT.Gelu_apprx_tanh)
             h.append(h_t)
+
+        for t in range(PACK - 1):
+            first_layer(t)
 
         gate2_t = keep.tile([P, 2, U], F32, name="gate2_t", tag="w1_raw")
         nc.sync.dma_start(out=gate2_t[:], in_=gate2.rearrange("d p r -> p d r"))
@@ -142,51 +159,96 @@ def tile_picked_hop2_gelu_p_kernel(
                 gate_t[:, d, first * P : last * P], ALU.mult,
             )
 
-        picked = {}
-        back01 = psum.tile([P, 2, 2, P], F32, name="back01", tag="acc")
-        back2 = psum.tile([P, 2, P], F32, name="back2", tag="acc")
-        back = [back01[:, 0], back01[:, 1], back2[:]]
+        early = [keep.tile([P, PACK, 3 * P], F32, name="early%d" % d) for d in range(2)]
+        late = [keep.tile([P, PACK, 2 * P], F32, name="late%d" % d) for d in range(2)]
+
+        def term(d, t, first, last):
+            if first == 3 or (first == 2 and t < 2):
+                return late[d][:, t, (first - 2) * P : (last - 2) * P]
+            return early[d][:, t, first * P : last * P]
+
+        def gather(t, first, last):
+            for d in range(2):
+                gather_term(term(d, t, first, last), t, d, first, last)
+
+        def add_turned(target, t, b):
+            for d in range(2):
+                nc.tensor.matmul(
+                    target, term(d, t, b, b + 1), ident[:],
+                    start=(d == 0), stop=(d == 1), is_transpose=True,
+                )
+
+        plain = [bank("plain%d" % d, 4 + d, [P, SPLIT, 2, P]) for d in range(2)]
+
+        def gather_plain(d, e):
+            nc.scalar.activation(term(d, e, 0, SPLIT), h[e][:].indirect(pos[d][:, : SPLIT * BLOCK]), ACT.Copy)
+            for b in range(SPLIT):
+                nc.tensor.transpose(plain[d][:, b, e, :], term(d, e, b, b + 1), ident[:])
+
+        def round_pairs(name, turned, count):
+            pairs = keep.tile([P, count, 2 * P], BF16, name=name, align_bytes=64)
+            nc.scalar.copy(pairs[:].rearrange("v b (p e) -> v b p e", e=2), turned[:].rearrange("v b e p -> v b p e"))
+            return pairs
+
+        turned2 = [bank("turned20", 7, [P, 1, 2, P])]
+        for t in range(2):
+            gather(t, 2, 4)
+            add_turned(turned2[0][:, 0, t, :], t, 2)
+        gather_plain(0, 0)
+        first_layer(PACK - 1)
+        gather_plain(0, 1)
+        for e in range(2):
+            gather_plain(1, e)
+        scaled = [late[b][:, 2:, P:].rearrange("v h (p e) -> v h p e", e=2) for b in range(SPLIT)]
+        woven = [[plain[d][:, b].rearrange("v e (h p) -> v h p e", h=2) for b in range(SPLIT)] for d in range(2)]
+        for b in range(SPLIT):
+            nc.scalar.activation(scaled[b], woven[0][b], ACT.Copy, scale=gate_col[0][:, b : b + 1])
+
+        turned01 = bank("turned01", 6, [P, SPLIT, 2, P])
+        turned2.append(bank("turned21", 2, [P, 1, 2, P]))
+        gather(2, 0, 3)
+        for b in range(SPLIT):
+            add_turned(turned01[:, b, 0, :], 2, b)
+        add_turned(turned2[1][:, 0, 0, :], 2, 2)
+        gather(3, 0, SPLIT)
+        for b in range(SPLIT):
+            add_turned(turned01[:, b, 1, :], 3, b)
+
+        gather(3, 2, 3)
+        add_turned(turned2[1][:, 0, 1, :], 3, 2)
+
+        back = [bank("back%d" % b, number, [P, 2, P]) for b, number in enumerate((3, 0, 1))]
+        for b in range(SPLIT):
+            pairs0 = keep.tile([P, 2 * P], BF16, name="pairs0%d" % b, align_bytes=64)
+            nc.vector.scalar_tensor_tensor(
+                pairs0[:].rearrange("v (h p e) -> v h p e", h=2, e=2), woven[1][b],
+                gate_col[1][:, b : b + 1], scaled[b], ALU.mult, ALU.add,
+            )
+            nc.tensor.transpose(back[b][:, 0, :], pairs0[:].bitcast(F32), ident[:])
+        pairs1 = round_pairs("pairs1", turned01, SPLIT)
+        for b in range(SPLIT):
+            nc.tensor.transpose(back[b][:, 1, :], pairs1[:, b, :].bitcast(F32), ident[:])
         for u in range(2):
-            for t in (2 * u, 2 * u + 1):
-                if t < PACK - 1:
-                    for d in range(2):
-                        term = keep.tile([P, TURNED * P], F32, name="term%d%d" % (t, d))
-                        gather_term(term[:], t, d, 0, TURNED)
-                        for b in range(TURNED):
-                            picked[t, d, b] = term[:, b * P : (b + 1) * P]
-                else:
-                    for b in range(TURNED):
-                        for d in range(2):
-                            term = keep.tile([P, P], F32, name="term%d%d%d" % (t, d, b), tag="late%d%d" % (d, b))
-                            gather_term(term[:], t, d, b, b + 1)
-                            picked[t, d, b] = term[:]
-            for b in range(TURNED):
-                turned = psum.tile([P, 2, P], F32, name="turned", tag="turned")
-                for e in range(2):
-                    for d in range(2):
-                        nc.tensor.matmul(
-                            turned[:, e, :], picked[2 * u + e, d, b], ident[:],
-                            start=(d == 0), stop=(d == 1), is_transpose=True,
-                        )
-                pairs = keep.tile([P, 2 * P], BF16, name="pairs%d%d" % (u, b), align_bytes=64)
-                nc.scalar.copy(pairs[:].rearrange("v (p e) -> v p e", e=2), turned[:].rearrange("v e p -> v p e"))
-                nc.tensor.transpose(back[b][:, u, :], pairs[:].bitcast(F32), ident[:])
-
-        zb01 = keep.tile([P, 2 * P * PACK], BF16, name="zb01", align_bytes=64)
-        zb2 = keep.tile([P, P * PACK], BF16, name="zb2", align_bytes=64)
-        nc.scalar.copy(
-            zb01[:].bitcast(F32).rearrange("p (b v u) -> p b v u", b=2, u=2), back01[:].rearrange("p b u v -> p b v u")
-        )
-        nc.scalar.copy(zb2[:].bitcast(F32).rearrange("p (v u) -> p v u", u=2), back2[:].rearrange("p u v -> p v u"))
-
-        direct = [keep.tile([P, PACK, P], F32, name="direct%d" % d, tag="late%d0" % d) for d in range(2)]
-        for d in range(2):
-            for t in range(PACK):
-                gather_term(direct[d][:, t, :], t, d, TURNED, TURNED + 1)
+            pairs2 = round_pairs("pairs2%d" % u, turned2[u], 1)
+            nc.tensor.transpose(back[2][:, u, :], pairs2[:, 0, :].bitcast(F32), ident[:])
+        zb = []
+        for b in range(3):
+            zb_b = keep.tile([P, P * PACK], BF16, name="zb%d" % b, align_bytes=64)
+            nc.scalar.copy(zb_b[:].bitcast(F32).rearrange("p (v u) -> p v u", u=2), back[b][:].rearrange("p u v -> p v u"))
+            zb.append(zb_b)
+        for d, t in ((0, 2), (0, 3), (1, 2)):
+            gather_term(term(d, t, 3, 4), t, d, 3, 4)
+        for i in range(2):
+            half = slice(P + i * P // 2, P + (i + 1) * P // 2)
+            nc.vector.tensor_tensor(
+                late[1][:, 3, half], h[3][:].indirect(pos[1][:, 3 * BLOCK + i * BLOCK // 2 : 3 * BLOCK + (i + 1) * BLOCK // 2]),
+                gate_t[:, 1, 3 * P + i * P // 2 : 3 * P + (i + 1) * P // 2], ALU.mult,
+            )
+        direct = [late[d][:, :, P:] for d in range(2)]
 
         g = keep.tile([P, V], F32, name="g")
 
-        def second_layer(zb, start, width, tag):
+        def second_layer(zb, start, width, tag, number):
             zc = keep.tile([P, width], U32, name="zc%d" % start, tag=tag, align_bytes=64)
             zs = keep.tile([P, width], U8, name="zs%d" % start, align_bytes=64)
             for c in range(0, width, P):
@@ -194,36 +256,39 @@ def tile_picked_hop2_gelu_p_kernel(
                 nc.vector.quantize_mx(
                     out=zc[:, c:end].bitcast(FP8X4), scales=zs[:, c:end], in_=zb[:, PACK * c : PACK * end]
                 )
-            acc2 = psum.tile([P, width], F32, name="acc2", tag="turned")
+            acc2 = bank("second%d" % start, number, [P, width])
             nc.tensor.matmul_mx(
                 out=acc2[:], lhsT=w2w[:].bitcast(FP8X4), lhsT_scale=w2s[:],
                 rhs=zc[:].bitcast(FP8X4), rhs_scale=zs[:], start=True, stop=True,
             )
             nc.scalar.activation(g[:, start : start + width], acc2[:], ACT.Relu)
 
-        second_layer(zb01[:], 0, 2 * P, "h2")
-        zb3 = zb01[:, : P * PACK]
+        for b, number in enumerate((2, 4, 5)):
+            second_layer(zb[b][:], b * P, P, "zc%d" % b, number)
         groups = P // 8
+        zb3 = []
         for i in range(2):
+            zb_half = keep.tile([P, P * PACK // 2], BF16, name="zb3%d" % i, align_bytes=64)
             nc.vector.tensor_tensor(
-                zb3.rearrange("p (c i t) -> p c t i", i=4, t=PACK)[:, groups * i : groups * (i + 1)],
-                direct[0][:].rearrange("p t (c i) -> p c t i", i=4)[:, groups * i : groups * (i + 1)],
-                direct[1][:].rearrange("p t (c i) -> p c t i", i=4)[:, groups * i : groups * (i + 1)],
+                zb_half[:].rearrange("p (c i t) -> p c t i", i=4, t=PACK),
+                direct[0].rearrange("p t (c i) -> p c t i", i=4)[:, groups * i : groups * (i + 1)],
+                direct[1].rearrange("p t (c i) -> p c t i", i=4)[:, groups * i : groups * (i + 1)],
                 ALU.add,
             )
-        second_layer(zb2[:], 2 * P, P, "zc2")
+            zb3.append(zb_half)
         for i in range(2):
-            second_layer(zb01[:, 2 * P * i : 2 * P * (i + 1)], TURNED * P + i * P // 2, P // 2, "zc3%d" % i)
+            second_layer(zb3[i][:], 3 * P + i * P // 2, P // 2, "zc3%d" % i, 6 + i)
 
+        plain1 = keep.tile([P, SHARED], F32, name="plain1")
         out0 = keep.tile([P, U], F32, name="out0")
+        out1 = keep.tile([P, U], F32, name="out1")
+        nc.scalar.activation(plain1[:], g[:].indirect(nxt[1][:, : SHARED // LIST]), ACT.Copy)
         nc.vector.tensor_tensor(out0[:], g[:].indirect(nxt[0][:]), gate2_t[:, 0, :], ALU.mult)
-        out1 = [keep.tile([P, P], F32, name="out1%d" % i) for i in range(2)]
-        for i in range(2):
-            nc.vector.tensor_tensor(
-                out1[i][:], g[:].indirect(nxt[1][:, BLOCK * i : BLOCK * (i + 1)]),
-                gate2_t[:, 1, P * i : P * (i + 1)], ALU.mult,
-            )
-        for i in range(2):
-            res = keep.tile([P, P], F32, name="res%d" % i)
-            nc.vector.tensor_tensor(res[:], out0[:, P * i : P * (i + 1)], out1[i][:], ALU.add)
-            nc.sync.dma_start(out=out[:, P * i : P * (i + 1)], in_=res[:])
+        nc.vector.tensor_tensor(
+            out1[:, SHARED:], g[:].indirect(nxt[1][:, SHARED // LIST :]), gate2_t[:, 1, SHARED:], ALU.mult
+        )
+        nc.vector.tensor_tensor(out1[:, :SHARED], plain1[:], gate2_t[:, 1, :SHARED], ALU.mult)
+        for name, part in (("own", slice(SHARED, U)), ("shared", slice(0, SHARED))):
+            res = keep.tile([P, part.stop - part.start], F32, name="res_" + name)
+            nc.vector.tensor_tensor(res[:], out0[:, part], out1[:, part], ALU.add)
+            nc.sync.dma_start(out=out[:, part], in_=res[:])

@@ -159,11 +159,12 @@ def tile_picked_hop2_gelu_p_kernel(
                 gate_t[:, d, first * P : last * P], ALU.mult,
             )
 
-        early = [keep.tile([P, PACK, 3 * P], F32, name="early%d" % d) for d in range(2)]
-        late = [keep.tile([P, PACK, 2 * P], F32, name="late%d" % d) for d in range(2)]
+        early = [keep.tile([P, PACK, SPLIT * P], F32, name="early%d" % d) for d in range(2)]
+        late_rows = [keep.tile([P, (2 * PACK + 1) * P], F32, name="late%d" % d) for d in range(2)]
+        late = [late_rows[d][:, : 2 * PACK * P].rearrange("p (t v) -> p t v", t=PACK) for d in range(2)]
 
         def term(d, t, first, last):
-            if first == 3 or (first == 2 and t < 2):
+            if first >= SPLIT:
                 return late[d][:, t, (first - 2) * P : (last - 2) * P]
             return early[d][:, t, first * P : last * P]
 
@@ -190,61 +191,55 @@ def tile_picked_hop2_gelu_p_kernel(
             nc.scalar.copy(pairs[:].rearrange("v b (p e) -> v b p e", e=2), turned[:].rearrange("v b e p -> v b p e"))
             return pairs
 
-        turned2 = [bank("turned20", 7, [P, 1, 2, P])]
         for t in range(2):
             gather(t, 2, 4)
-            add_turned(turned2[0][:, 0, t, :], t, 2)
-        gather_plain(0, 0)
         first_layer(PACK - 1)
-        gather_plain(0, 1)
-        for e in range(2):
-            gather_plain(1, e)
-        scaled = [late[b][:, 2:, P:].rearrange("v h (p e) -> v h p e", e=2) for b in range(SPLIT)]
-        woven = [[plain[d][:, b].rearrange("v e (h p) -> v h p e", h=2) for b in range(SPLIT)] for d in range(2)]
+        for d in range(2):
+            for e in range(2):
+                gather_plain(d, e)
+        scaled0 = keep.tile([P, 2 * P], F32, name="scaled0", tag="zb2", align_bytes=64)
+        scaled = [view.rearrange("v (p e) -> v p e", e=2) for view in (scaled0[:], late_rows[1][:, (2 * PACK - 1) * P :])]
+        woven = [[plain[d][:, b].rearrange("v e p -> v p e") for b in range(SPLIT)] for d in range(2)]
         for b in range(SPLIT):
             nc.scalar.activation(scaled[b], woven[0][b], ACT.Copy, scale=gate_col[0][:, b : b + 1])
 
         turned01 = bank("turned01", 6, [P, SPLIT, 2, P])
-        turned2.append(bank("turned21", 2, [P, 1, 2, P]))
-        gather(2, 0, 3)
-        for b in range(SPLIT):
-            add_turned(turned01[:, b, 0, :], 2, b)
-        add_turned(turned2[1][:, 0, 0, :], 2, 2)
-        gather(3, 0, SPLIT)
-        for b in range(SPLIT):
-            add_turned(turned01[:, b, 1, :], 3, b)
+        for e in range(2):
+            gather(2 + e, 0, SPLIT)
+            for b in range(SPLIT):
+                add_turned(turned01[:, b, e, :], 2 + e, b)
+        gather(2, SPLIT, PACK)
+        gather_term(term(0, 3, 2, 4), 3, 0, 2, 4)
+        gather_term(term(1, 3, 2, 3), 3, 1, 2, 3)
 
-        gather(3, 2, 3)
-        add_turned(turned2[1][:, 0, 1, :], 3, 2)
-
-        back = [bank("back%d" % b, number, [P, 2, P]) for b, number in enumerate((3, 0, 1))]
+        back = [bank("back%d" % b, number, [P, 2, P]) for b, number in enumerate((3, 0))]
         for b in range(SPLIT):
             pairs0 = keep.tile([P, 2 * P], BF16, name="pairs0%d" % b, align_bytes=64)
             nc.vector.scalar_tensor_tensor(
-                pairs0[:].rearrange("v (h p e) -> v h p e", h=2, e=2), woven[1][b],
+                pairs0[:].rearrange("v (p e) -> v p e", e=2), woven[1][b],
                 gate_col[1][:, b : b + 1], scaled[b], ALU.mult, ALU.add,
             )
             nc.tensor.transpose(back[b][:, 0, :], pairs0[:].bitcast(F32), ident[:])
         pairs1 = round_pairs("pairs1", turned01, SPLIT)
         for b in range(SPLIT):
             nc.tensor.transpose(back[b][:, 1, :], pairs1[:, b, :].bitcast(F32), ident[:])
-        for u in range(2):
-            pairs2 = round_pairs("pairs2%d" % u, turned2[u], 1)
-            nc.tensor.transpose(back[2][:, u, :], pairs2[:, 0, :].bitcast(F32), ident[:])
         zb = []
-        for b in range(3):
+        for b in range(SPLIT):
             zb_b = keep.tile([P, P * PACK], BF16, name="zb%d" % b, align_bytes=64)
             nc.scalar.copy(zb_b[:].bitcast(F32).rearrange("p (v u) -> p v u", u=2), back[b][:].rearrange("p u v -> p v u"))
             zb.append(zb_b)
-        for d, t in ((0, 2), (0, 3), (1, 2)):
-            gather_term(term(d, t, 3, 4), t, d, 3, 4)
         for i in range(2):
-            half = slice(P + i * P // 2, P + (i + 1) * P // 2)
             nc.vector.tensor_tensor(
-                late[1][:, 3, half], h[3][:].indirect(pos[1][:, 3 * BLOCK + i * BLOCK // 2 : 3 * BLOCK + (i + 1) * BLOCK // 2]),
+                late[1][:, 3, P + i * P // 2 : P + (i + 1) * P // 2],
+                h[3][:].indirect(pos[1][:, 3 * BLOCK + i * BLOCK // 2 : 3 * BLOCK + (i + 1) * BLOCK // 2]),
                 gate_t[:, 1, 3 * P + i * P // 2 : 3 * P + (i + 1) * P // 2], ALU.mult,
             )
-        direct = [late[d][:, :, P:] for d in range(2)]
+
+        def add_direct(name, start, width):
+            zb_part = keep.tile([P, width * PACK], BF16, name=name, tag=name, align_bytes=64)
+            views = [late[d][:, :, start : start + width].rearrange("p t (c i) -> p c t i", i=4) for d in range(2)]
+            nc.vector.tensor_tensor(zb_part[:].rearrange("p (c i t) -> p c t i", i=4, t=PACK), views[0], views[1], ALU.add)
+            return zb_part
 
         g = keep.tile([P, V], F32, name="g")
 
@@ -263,21 +258,14 @@ def tile_picked_hop2_gelu_p_kernel(
             )
             nc.scalar.activation(g[:, start : start + width], acc2[:], ACT.Relu)
 
-        for b, number in enumerate((2, 4, 5)):
+        for b, number in enumerate((2, 4)):
             second_layer(zb[b][:], b * P, P, "zc%d" % b, number)
-        groups = P // 8
-        zb3 = []
-        for i in range(2):
-            zb_half = keep.tile([P, P * PACK // 2], BF16, name="zb3%d" % i, align_bytes=64)
-            nc.vector.tensor_tensor(
-                zb_half[:].rearrange("p (c i t) -> p c t i", i=4, t=PACK),
-                direct[0].rearrange("p t (c i) -> p c t i", i=4)[:, groups * i : groups * (i + 1)],
-                direct[1].rearrange("p t (c i) -> p c t i", i=4)[:, groups * i : groups * (i + 1)],
-                ALU.add,
-            )
-            zb3.append(zb_half)
-        for i in range(2):
-            second_layer(zb3[i][:], 3 * P + i * P // 2, P // 2, "zc3%d" % i, 6 + i)
+        zb2 = add_direct("zb2", 0, P)
+        zb30 = add_direct("zb30", P, P // 2)
+        second_layer(zb2[:], 2 * P, P, "zc2", 5)
+        zb31 = add_direct("zb31", P + P // 2, P // 2)
+        second_layer(zb30[:], 3 * P, P // 2, "zc30", 6)
+        second_layer(zb31[:], 3 * P + P // 2, P // 2, "zc31", 7)
 
         plain1 = keep.tile([P, SHARED], F32, name="plain1")
         out0 = keep.tile([P, U], F32, name="out0")

@@ -237,8 +237,8 @@ def tile_picked_hop2_gelu_p_kernel(
 
         def add_direct(name, start, width):
             zb_part = keep.tile([P, width * PACK], BF16, name=name, tag=name, align_bytes=64)
-            views = [late[d][:, :, start : start + width].rearrange("p t (c i) -> p c t i", i=4) for d in range(2)]
-            nc.vector.tensor_tensor(zb_part[:].rearrange("p (c i t) -> p c t i", i=4, t=PACK), views[0], views[1], ALU.add)
+            views = [late[d][:, :, start : start + width].rearrange("p t (c i) -> p c t i", i=2) for d in range(2)]
+            nc.vector.tensor_tensor(zb_part[:].rearrange("p (c i t) -> p c t i", i=2, t=PACK), views[0], views[1], ALU.add)
             return zb_part
 
         g = keep.tile([P, V], F32, name="g")

@@ -147,7 +147,7 @@ def tile_picked_hop2_gelu_p_kernel(
                 nc.scalar.activation(h_t[:, start : start + width], acc[:], ACT.Gelu_apprx_tanh)
             h.append(h_t)
 
-        for t in range(PACK - 1):
+        for t in range(PACK):
             first_layer(t)
 
         gate2_t = keep.tile([P, 2, U], F32, name="gate2_t", tag="w1_raw")
@@ -159,87 +159,58 @@ def tile_picked_hop2_gelu_p_kernel(
                 gate_t[:, d, first * P : last * P], ALU.mult,
             )
 
-        early = [keep.tile([P, PACK, SPLIT * P], F32, name="early%d" % d) for d in range(2)]
-        late_rows = [keep.tile([P, (2 * PACK + 1) * P], F32, name="late%d" % d) for d in range(2)]
-        late = [late_rows[d][:, : 2 * PACK * P].rearrange("p (t v) -> p t v", t=PACK) for d in range(2)]
+        split_cols = SPLIT * P
+        terms = [keep.tile([P, PACK, V], F32, name="terms%d" % d) for d in range(2)]
 
-        def term(d, t, first, last):
-            if first >= SPLIT:
-                return late[d][:, t, (first - 2) * P : (last - 2) * P]
-            return early[d][:, t, first * P : last * P]
-
-        def gather(t, first, last):
+        turned = [bank("turned%d" % b, 6 + b, [P, 2, P]) for b in range(SPLIT)]
+        for t in range(2):
             for d in range(2):
-                gather_term(term(d, t, first, last), t, d, first, last)
-
-        def add_turned(target, t, b):
-            for d in range(2):
-                nc.tensor.matmul(
-                    target, term(d, t, b, b + 1), ident[:],
-                    start=(d == 0), stop=(d == 1), is_transpose=True,
-                )
+                gather_term(terms[d][:, t, :], t, d, 0, PACK)
+            for b in range(SPLIT):
+                for d in range(2):
+                    nc.tensor.matmul(
+                        turned[b][:, t, :], terms[d][:, t, b * P : (b + 1) * P], ident[:],
+                        start=(d == 0), stop=(d == 1), is_transpose=True,
+                    )
 
         plain = [bank("plain%d" % d, 4 + d, [P, SPLIT, 2, P]) for d in range(2)]
-
-        def gather_plain(d, e):
-            nc.scalar.activation(term(d, e, 0, SPLIT), h[e][:].indirect(pos[d][:, : SPLIT * BLOCK]), ACT.Copy)
-            for b in range(SPLIT):
-                nc.tensor.transpose(plain[d][:, b, e, :], term(d, e, b, b + 1), ident[:])
-
-        def round_pairs(name, turned, count):
-            pairs = keep.tile([P, count, 2 * P], BF16, name=name, align_bytes=64)
-            nc.scalar.copy(pairs[:].rearrange("v b (p e) -> v b p e", e=2), turned[:].rearrange("v b e p -> v b p e"))
-            return pairs
-
-        for t in range(2):
-            gather(t, 2, 4)
-        first_layer(PACK - 1)
         for d in range(2):
             for e in range(2):
-                gather_plain(d, e)
-        scaled0 = keep.tile([P, 2 * P], F32, name="scaled0", tag="zb2", align_bytes=64)
-        scaled = [view.rearrange("v (p e) -> v p e", e=2) for view in (scaled0[:], late_rows[1][:, (2 * PACK - 1) * P :])]
-        woven = [[plain[d][:, b].rearrange("v e p -> v p e") for b in range(SPLIT)] for d in range(2)]
-        for b in range(SPLIT):
-            nc.scalar.activation(scaled[b], woven[0][b], ACT.Copy, scale=gate_col[0][:, b : b + 1])
+                nc.scalar.activation(
+                    terms[d][:, 2 + e, :split_cols], h[2 + e][:].indirect(pos[d][:, : SPLIT * BLOCK]), ACT.Copy
+                )
+                for b in range(SPLIT):
+                    nc.tensor.transpose(plain[d][:, b, e, :], terms[d][:, 2 + e, b * P : (b + 1) * P], ident[:])
+        for t in (2, 3):
+            for d in range(2):
+                gather_term(terms[d][:, t, split_cols:], t, d, SPLIT, PACK)
 
-        turned01 = bank("turned01", 6, [P, SPLIT, 2, P])
-        for e in range(2):
-            gather(2 + e, 0, SPLIT)
-            for b in range(SPLIT):
-                add_turned(turned01[:, b, e, :], 2 + e, b)
-        gather(2, SPLIT, PACK)
-        gather_term(term(0, 3, 2, 4), 3, 0, 2, 4)
-        gather_term(term(1, 3, 2, 3), 3, 1, 2, 3)
+        woven = [[plain[d][:, b].rearrange("v e p -> v p e") for b in range(SPLIT)] for d in range(2)]
+        scaled = []
+        for b, tag in enumerate(("zb2", "zb3")):
+            first = keep.tile([P, P, 2], F32, name="scaled%d" % b, tag=tag, align_bytes=64)
+            nc.scalar.activation(first[:], woven[0][b], ACT.Copy, scale=gate_col[0][:, b : b + 1])
+            scaled.append(first)
 
         back = [bank("back%d" % b, number, [P, 2, P]) for b, number in enumerate((3, 0))]
         for b in range(SPLIT):
-            pairs0 = keep.tile([P, 2 * P], BF16, name="pairs0%d" % b, align_bytes=64)
-            nc.vector.scalar_tensor_tensor(
-                pairs0[:].rearrange("v (p e) -> v p e", e=2), woven[1][b],
-                gate_col[1][:, b : b + 1], scaled[b], ALU.mult, ALU.add,
-            )
-            nc.tensor.transpose(back[b][:, 0, :], pairs0[:].bitcast(F32), ident[:])
-        pairs1 = round_pairs("pairs1", turned01, SPLIT)
-        for b in range(SPLIT):
-            nc.tensor.transpose(back[b][:, 1, :], pairs1[:, b, :].bitcast(F32), ident[:])
+            pairs0 = keep.tile([P, P, 2], BF16, name="pairs0%d" % b, align_bytes=64)
+            nc.scalar.copy(pairs0[:], turned[b][:].rearrange("v e p -> v p e"))
+            nc.tensor.transpose(back[b][:, 0, :], pairs0[:].rearrange("v p e -> v (p e)").bitcast(F32), ident[:])
         zb = []
         for b in range(SPLIT):
+            pairs1 = keep.tile([P, P, 2], BF16, name="pairs1%d" % b, align_bytes=64)
+            nc.vector.scalar_tensor_tensor(
+                pairs1[:], woven[1][b], gate_col[1][:, b : b + 1], scaled[b][:], ALU.mult, ALU.add
+            )
+            nc.tensor.transpose(back[b][:, 1, :], pairs1[:].rearrange("v p e -> v (p e)").bitcast(F32), ident[:])
             zb_b = keep.tile([P, P * PACK], BF16, name="zb%d" % b, align_bytes=64)
             nc.scalar.copy(zb_b[:].bitcast(F32).rearrange("p (v u) -> p v u", u=2), back[b][:].rearrange("p u v -> p v u"))
             zb.append(zb_b)
-        for i in range(2):
-            nc.vector.tensor_tensor(
-                late[1][:, 3, P + i * P // 2 : P + (i + 1) * P // 2],
-                h[3][:].indirect(pos[1][:, 3 * BLOCK + i * BLOCK // 2 : 3 * BLOCK + (i + 1) * BLOCK // 2]),
-                gate_t[:, 1, 3 * P + i * P // 2 : 3 * P + (i + 1) * P // 2], ALU.mult,
-            )
 
-        def add_direct(name, start, width):
-            zb_part = keep.tile([P, width * PACK], BF16, name=name, tag=name, align_bytes=64)
-            views = [late[d][:, :, start : start + width].rearrange("p t (c i) -> p c t i", i=2) for d in range(2)]
-            nc.vector.tensor_tensor(zb_part[:].rearrange("p (c i t) -> p c t i", i=2, t=PACK), views[0], views[1], ALU.add)
-            return zb_part
+        def add_direct(zb_part, start, width):
+            views = [terms[d][:, :, start : start + width].rearrange("p t (c i) -> p c t i", i=2) for d in range(2)]
+            nc.vector.tensor_tensor(zb_part.rearrange("p (c i t) -> p c t i", i=2, t=PACK), views[0], views[1], ALU.add)
 
         g = keep.tile([P, V], F32, name="g")
 
@@ -260,12 +231,14 @@ def tile_picked_hop2_gelu_p_kernel(
 
         for b, number in enumerate((2, 4)):
             second_layer(zb[b][:], b * P, P, "zc%d" % b, number)
-        zb2 = add_direct("zb2", 0, P)
-        zb30 = add_direct("zb30", P, P // 2)
+        zb2 = keep.tile([P, P * PACK], BF16, name="zb2", tag="zb2", align_bytes=64)
+        zb3 = keep.tile([P, P * PACK], BF16, name="zb3", tag="zb3", align_bytes=64)
+        add_direct(zb2[:], 2 * P, P)
+        add_direct(zb3[:, : 2 * P], 3 * P, P // 2)
         second_layer(zb2[:], 2 * P, P, "zc2", 5)
-        zb31 = add_direct("zb31", P + P // 2, P // 2)
-        second_layer(zb30[:], 3 * P, P // 2, "zc30", 6)
-        second_layer(zb31[:], 3 * P + P // 2, P // 2, "zc31", 7)
+        add_direct(zb3[:, 2 * P :], 3 * P + P // 2, P // 2)
+        second_layer(zb3[:, : 2 * P], 3 * P, P // 2, "zc30", 6)
+        second_layer(zb3[:, 2 * P :], 3 * P + P // 2, P // 2, "zc31", 7)
 
         plain1 = keep.tile([P, SHARED], F32, name="plain1")
         out0 = keep.tile([P, U], F32, name="out0")

@@ -229,8 +229,6 @@ def tile_picked_hop2_gelu_p_kernel(
             )
             nc.scalar.activation(g[:, start : start + width], acc2[:], ACT.Relu)
 
-        for b, number in enumerate((2, 4)):
-            second_layer(zb[b][:], b * P, P, "zc%d" % b, number)
         zb2 = keep.tile([P, P * PACK], BF16, name="zb2", tag="zb2", align_bytes=64)
         zb3 = keep.tile([P, P * PACK], BF16, name="zb3", tag="zb3", align_bytes=64)
         add_direct(zb2[:], 2 * P, P)
@@ -238,7 +236,9 @@ def tile_picked_hop2_gelu_p_kernel(
         second_layer(zb2[:], 2 * P, P, "zc2", 5)
         add_direct(zb3[:, 2 * P :], 3 * P + P // 2, P // 2)
         second_layer(zb3[:, : 2 * P], 3 * P, P // 2, "zc30", 6)
+        second_layer(zb[0][:], 0, P, "zc0", 2)
         second_layer(zb3[:, 2 * P :], 3 * P + P // 2, P // 2, "zc31", 7)
+        second_layer(zb[1][:], P, P, "zc1", 4)
 
         plain1 = keep.tile([P, SHARED], F32, name="plain1")
         out0 = keep.tile([P, U], F32, name="out0")

@@ -25,8 +25,7 @@ SPLIT = 2
 SHARED = 160
 X_AHEAD = 1024
 W1_AHEAD = 1408
-FIRST_SHARE = 96
-LATER_SHARE = 100
+OVERLAP = 8
 
 
 def tile_picked_hop2_gelu_p_kernel(
@@ -108,7 +107,7 @@ def tile_picked_hop2_gelu_p_kernel(
 
         def deal(copy, dealt, columns, rows, planes):
             copy(
-                dealt[:].rearrange("p (t m j) -> p m j t", m=P, j=PACK)[:, columns, rows, :],
+                dealt.rearrange("p (t m j) -> p m j t", m=P, j=PACK)[:, columns, rows, :],
                 w1_raw[:].rearrange("p (j m t) -> p m j t", j=PACK, t=PACK)[:, columns, rows, planes],
             )
 
@@ -118,15 +117,20 @@ def tile_picked_hop2_gelu_p_kernel(
             nc.vector.quantize_mx(out=codes[:].bitcast(FP8X4), scales=scales[:], in_=source)
             return [(codes[:, e * P : (e + 1) * P], scales[:, e * P : (e + 1) * P]) for e in range(count)]
 
-        dealt0 = keep.tile([P, P * PACK], BF16, name="dealt0", tag="dealt", align_bytes=64)
-        deal(nc.scalar.copy, dealt0, slice(0, P), slice(0, 2), slice(0, 1))
-        deal(nc.scalar.copy, dealt0, slice(FIRST_SHARE, P), slice(2, PACK), slice(0, 1))
-        deal(nc.vector.tensor_copy, dealt0, slice(0, FIRST_SHARE), slice(2, PACK), slice(0, 1))
-        w1q = quantise_w1(dealt0[:], "0", 1)
-        others = keep.tile([P, 3 * P * PACK], BF16, name="others", tag="dealt", align_bytes=64)
-        deal(nc.scalar.copy, others, slice(LATER_SHARE, P), slice(0, PACK), slice(1, PACK))
-        deal(nc.vector.tensor_copy, others, slice(0, LATER_SHARE), slice(0, PACK), slice(1, PACK))
-        w1q = w1q + quantise_w1(others[:, : P * PACK], "1", 1) + quantise_w1(others[:, P * PACK :], "23", 2)
+        plane = P * PACK
+        dealt = keep.tile([P, PACK * plane - OVERLAP * PACK], BF16, name="dealt", align_bytes=64)
+        dealt0 = dealt[:, :plane]
+        others = dealt[:, plane - OVERLAP * PACK :]
+        low, high = slice(0, 2), slice(2, PACK)
+        deal(nc.scalar.copy, dealt0, slice(0, P), low, slice(0, 1))
+        deal(nc.scalar.copy, others, slice(OVERLAP, P), low, slice(1, PACK))
+        deal(nc.vector.tensor_copy, dealt0, slice(0, P), high, slice(0, 1))
+        w1q = quantise_w1(dealt0, "0", 1)
+        deal(nc.scalar.copy, others[:, 2 * plane :], slice(0, P), high, slice(3, PACK))
+        deal(nc.vector.tensor_copy, others, slice(0, OVERLAP), low, slice(1, PACK))
+        deal(nc.vector.tensor_copy, others[:, : 2 * plane], slice(0, P), high, slice(1, 3))
+        last = quantise_w1(others[:, 2 * plane :], "3", 1)
+        w1q = w1q + quantise_w1(others[:, :plane], "1", 1) + quantise_w1(others[:, plane : 2 * plane], "2", 1) + last
 
         h = []
         products = []

@@ -95,13 +95,6 @@ def tile_picked_hop2_gelu_p_kernel(
             nc.vector.tensor_copy(gw_half[:], xw[:].bitcast(U32).indirect(entries))
             gw.append(gw_half)
 
-        for i in range(2):
-            idle = bank("idle%d" % i, 4 + i, [P, BANK])
-            nc.tensor.matmul_mx(
-                out=idle[:], lhsT=gw[0][:, :P].bitcast(FP8X4), lhsT_scale=gs_raw[:, :P],
-                rhs=gw[0][:].bitcast(FP8X4), rhs_scale=gs_raw[:, :BANK], start=True, stop=True,
-            )
-
         w2w = keep.tile([P, N], I32, name="w2w", tag="gs_raw", align_bytes=64)
         nc.sync.dma_start(out=w2w[:], in_=w2_words[0].rearrange("p n t -> p (n t)").bitcast(I32))
 

@@ -104,10 +104,16 @@ def tile_picked_hop2_gelu_p_kernel(
                 w1_raw[:].rearrange("p (j m t) -> p m j t", j=PACK, t=PACK)[:, columns, rows, planes],
             )
 
-        def quantise_w1(source, name, count):
+        def quantise_w1(source, name, count, pieces=1):
             codes = keep.tile([P, count * P], U32, name="w1c" + name, align_bytes=64)
             scales = keep.tile([P, count * P], U8, name="w1s" + name, align_bytes=64)
-            nc.vector.quantize_mx(out=codes[:].bitcast(FP8X4), scales=scales[:], in_=source)
+            width = count * P // pieces
+            for i in range(pieces):
+                part = slice(i * width, (i + 1) * width)
+                nc.vector.quantize_mx(
+                    out=codes[:, part].bitcast(FP8X4), scales=scales[:, part],
+                    in_=source[:, PACK * i * width : PACK * (i + 1) * width],
+                )
             return [(codes[:, e * P : (e + 1) * P], scales[:, e * P : (e + 1) * P]) for e in range(count)]
 
         plane = P * PACK
@@ -117,8 +123,9 @@ def tile_picked_hop2_gelu_p_kernel(
         low, high = slice(0, 2), slice(2, PACK)
         deal(nc.scalar.copy, dealt0, slice(0, P), low, slice(0, 1))
         deal(nc.scalar.copy, others, slice(OVERLAP, P), low, slice(1, PACK))
-        deal(nc.vector.tensor_copy, dealt0, slice(0, P), high, slice(0, 1))
-        w1q = quantise_w1(dealt0, "0", 1)
+        for i in range(2):
+            deal(nc.vector.tensor_copy, dealt0, slice(i * P // 2, (i + 1) * P // 2), high, slice(0, 1))
+        w1q = quantise_w1(dealt0, "0", 1, pieces=2)
         deal(nc.scalar.copy, others[:, 2 * plane :], slice(0, P), high, slice(3, PACK))
         deal(nc.vector.tensor_copy, others, slice(0, OVERLAP), low, slice(1, PACK))
         deal(nc.vector.tensor_copy, others[:, : 2 * plane], slice(0, P), high, slice(1, 3))

@@ -253,7 +253,7 @@ def tile_picked_hop2_gelu_p_kernel(
             out1[:, SHARED:], g[:].indirect(nxt[1][:, SHARED // LIST :]), gate2_t[:, 1, SHARED:], ALU.mult
         )
         nc.vector.tensor_tensor(out1[:, :SHARED], plain1[:], gate2_t[:, 1, :SHARED], ALU.mult)
-        for name, part in (("own", slice(SHARED, U)), ("shared", slice(0, SHARED))):
-            res = keep.tile([P, part.stop - part.start], F32, name="res_" + name)
-            nc.vector.tensor_tensor(res[:], out0[:, part], out1[:, part], ALU.add)
-            nc.sync.dma_start(out=out[:, part], in_=res[:])
+        res = keep.tile([P, U], F32, name="res")
+        for part in (slice(SHARED, U), slice(0, SHARED)):
+            nc.vector.tensor_tensor(res[:, part], out0[:, part], out1[:, part], ALU.add)
+        nc.sync.dma_start(out=out, in_=res[:])

@@ -25,6 +25,7 @@ SPLIT = 2
 SHARED = 160
 X_AHEAD = 1024
 W1_AHEAD = 1408
+MOVES_AHEAD = 2
 OVERLAP = 8
 
 
@@ -73,8 +74,9 @@ def tile_picked_hop2_gelu_p_kernel(
         gs_raw = keep.tile([P, S], U8, name="gs_raw", tag="gs_raw", align_bytes=64)
         nc.vector.tensor_copy(gs_raw[:], xs[:].indirect(offs_t[:]))
         for r in range(PACK):
+            if r == MOVES_AHEAD:
+                nc.sync.dma_start(out=w1_raw[:, W1_AHEAD:], in_=w1_rows[:, W1_AHEAD:])
             nc.sync.dma_start(out=gs[:].bitcast(I32)[r:P:32, :], in_=gs_raw[:].bitcast(I32)[32 + 4 * r : 96 : 16, :])
-        nc.sync.dma_start(out=w1_raw[:, W1_AHEAD:], in_=w1_rows[:, W1_AHEAD:])
 
         pos = [load_list("pos1_t", pos1, V), load_list("pos2_t", pos2, V)]
         gate_t = over.tile([P, 2, V], F32, name="gate_t", offset=N, align_bytes=64)

from contextlib import ExitStack

import concourse.mybir as mybir
from concourse.masks import make_identity

K, T, S, V, H, N, U = 512, 4096, 1024, 512, 512, 128, 256
FLOPS = 2 * K * H * S + 2 * H * N * V

F32 = mybir.dt.float32
BF16 = mybir.dt.bfloat16
I32 = mybir.dt.int32
U32 = mybir.dt.uint32
U16 = mybir.dt.uint16
U8 = mybir.dt.uint8
FP8X4 = mybir.dt.float8_e4m3fn_x4
ACT = mybir.ActivationFunctionType
ALU = mybir.AluOpType

P = 128
PACK = 4
BANK = 512
LIST = 16
BLOCK = P // LIST
SPLIT = 2
SHARED = 160
X_AHEAD = 1024
W1_AHEAD = 1408
MOVES_AHEAD = 2
OVERLAP = 8


def tile_picked_hop2_gelu_p_kernel(
    tc, x_words, x_scales, w1, w2_words, w2_scales, gate, gate2, offs, pos1, pos2, nxt1, nxt2, out
):
    nc = tc.nc
    with ExitStack() as ctx:
        lists = ctx.enter_context(tc.tile_pool(name="lists", bufs=1))
        keep = ctx.enter_context(tc.tile_pool(name="keep", bufs=1))
        psum = ctx.enter_context(tc.psum_pool(name="psum", bufs=1))

        def bank(name, number, shape):
            return psum.tile(shape, F32, name=name, tag="bank%d" % number)

        over = ctx.enter_context(tc.tile_pool(name="over", bufs=1))

        xs = over.tile([P, T], U8, name="xs", offset=0, align_bytes=64)
        nc.vector.memset(xs[:].bitcast(I32), 0)
        ident = keep.tile([P, P], F32, name="ident")
        nc.vector.memset(ident[:], 0.0)
        make_identity(nc, ident[:], nomemset=True)
        gs = keep.tile([P, S], U8, name="gs", align_bytes=64)
        nc.vector.memset(gs[:].bitcast(I32), 0)
        w2s = keep.tile([P, N], U8, name="w2s", align_bytes=64)
        nc.vector.memset(w2s[:].bitcast(I32), 0)

        def load_list(name, src, entries):
            list_tile = lists.tile([P, entries // LIST], U16, name=name)
            nc.sync.dma_start(list_tile[:], src)
            return list_tile

        x_rows = x_words[0].rearrange("p n t -> p (n t)").bitcast(I32)
        xw = keep.tile([P, T], I32, name="xw", align_bytes=64)
        nc.sync.dma_start(out=xw[:, :X_AHEAD], in_=x_rows[:, :X_AHEAD])
        offs_t = load_list("offs_t", offs, S)
        nc.sync.dma_start(out=xs[:].bitcast(I32)[32:96:4, :], in_=x_scales[0].bitcast(I32))
        nc.sync.dma_start(out=xw[:, X_AHEAD:], in_=x_rows[:, X_AHEAD:])
        w1_rows = w1.rearrange("(p j) c -> p (j c)", j=PACK)
        w1_raw = keep.tile([P, PACK * H], F32, name="w1_raw")
        nc.sync.dma_start(out=w1_raw[:, :W1_AHEAD], in_=w1_rows[:, :W1_AHEAD])

        warm = keep.tile([P, 1], F32, name="warm")
        nc.scalar.activation(warm[:], ident[:, 0:1], ACT.Gelu_apprx_tanh)

        gs_raw = keep.tile([P, S], U8, name="gs_raw", tag="gs_raw", align_bytes=64)
        nc.vector.tensor_copy(gs_raw[:], xs[:].indirect(offs_t[:]))
        for r in range(PACK):
            if r == MOVES_AHEAD:
                nc.sync.dma_start(out=w1_raw[:, W1_AHEAD:], in_=w1_rows[:, W1_AHEAD:])
            nc.sync.dma_start(out=gs[:].bitcast(I32)[r:P:32, :], in_=gs_raw[:].bitcast(I32)[32 + 4 * r : 96 : 16, :])

        pos = [load_list("pos1_t", pos1, V), load_list("pos2_t", pos2, V)]
        gate_t = over.tile([P, 2, V], F32, name="gate_t", offset=N, align_bytes=64)
        nc.sync.dma_start(out=gate_t[:], in_=gate.rearrange("d p v -> p d v"))
        gate_col = []
        for d in range(2):
            col = keep.tile([P, SPLIT], F32, name="gate_col%d" % d)
            with nc.allow_non_contiguous_dma(reason="one gate value a partition"):
                nc.sync.dma_start(out=col[:], in_=gate[d, 0, : SPLIT * P].rearrange("(b v) -> v b", v=P))
            gate_col.append(col)
        nxt = [load_list("nxt1_t", nxt1, U), load_list("nxt2_t", nxt2, U)]
        for r in range(PACK):
            nc.sync.dma_start(out=w2s[:].bitcast(I32)[r:P:32, :], in_=w2_scales[0].bitcast(I32)[r:16:PACK, :])
        gw = []
        for half in range(2):
            gw_half = keep.tile([P, BANK], U32, name="gw%d" % half, align_bytes=64)
            entries = offs_t[:, half * BANK // LIST : (half + 1) * BANK // LIST]
            nc.vector.tensor_copy(gw_half[:], xw[:].bitcast(U32).indirect(entries))
            gw.append(gw_half)

        w2w = keep.tile([P, N], I32, name="w2w", tag="gs_raw", align_bytes=64)
        nc.sync.dma_start(out=w2w[:], in_=w2_words[0].rearrange("p n t -> p (n t)").bitcast(I32))

        def deal(copy, dealt, columns, rows, planes):
            copy(
                dealt.rearrange("p (t m j) -> p m j t", m=P, j=PACK)[:, columns, rows, :],
                w1_raw[:].rearrange("p (j m t) -> p m j t", j=PACK, t=PACK)[:, columns, rows, planes],
            )

        def quantise_w1(source, name, count, pieces=1):
            codes = keep.tile([P, count * P], U32, name="w1c" + name, align_bytes=64)
            scales = keep.tile([P, count * P], U8, name="w1s" + name, align_bytes=64)
            width = count * P // pieces
            for i in range(pieces):
                part = slice(i * width, (i + 1) * width)
                nc.vector.quantize_mx(
                    out=codes[:, part].bitcast(FP8X4), scales=scales[:, part],
                    in_=source[:, PACK * i * width : PACK * (i + 1) * width],
                )
            return [(codes[:, e * P : (e + 1) * P], scales[:, e * P : (e + 1) * P]) for e in range(count)]

        plane = P * PACK
        dealt = keep.tile([P, PACK * plane - OVERLAP * PACK], BF16, name="dealt", align_bytes=64)
        dealt0 = dealt[:, :plane]
        others = dealt[:, plane - OVERLAP * PACK :]
        low, high = slice(0, 2), slice(2, PACK)
        deal(nc.scalar.copy, dealt0, slice(0, P), low, slice(0, 1))
        deal(nc.scalar.copy, others, slice(OVERLAP, P), low, slice(1, PACK))
        for i in range(2):
            deal(nc.vector.tensor_copy, dealt0, slice(i * P // 2, (i + 1) * P // 2), high, slice(0, 1))
        w1q = quantise_w1(dealt0, "0", 1, pieces=2)
        deal(nc.scalar.copy, others[:, 2 * plane :], slice(0, P), high, slice(3, PACK))
        deal(nc.vector.tensor_copy, others, slice(0, OVERLAP), low, slice(1, PACK))
        deal(nc.vector.tensor_copy, others[:, : 2 * plane], slice(0, P), high, slice(1, 3))
        last = quantise_w1(others[:, 2 * plane :], "3", 1)
        w1q = w1q + quantise_w1(others[:, :plane], "1", 1) + quantise_w1(others[:, plane : 2 * plane], "2", 1) + last

        h = []
        products = []

        def first_layer(t):
            w1c, w1s = w1q[t]
            h_t = keep.tile([P, S], F32, name="h%d" % t, align_bytes=64)
            width = BANK // 2 if t == 0 else BANK
            for start in range(0, S, width):
                acc = bank("acc%d" % len(products), len(products) % 4, [P, width])
                products.append(acc)
                nc.tensor.matmul_mx(
                    out=acc[:], lhsT=w1c.bitcast(FP8X4), lhsT_scale=w1s,
                    rhs=gw[start // BANK][:, start % BANK : start % BANK + width].bitcast(FP8X4),
                    rhs_scale=gs[:, start : start + width],
                    start=True, stop=True,
                )
                nc.scalar.activation(h_t[:, start : start + width], acc[:], ACT.Gelu_apprx_tanh)
            h.append(h_t)

        for t in range(PACK):
            first_layer(t)

        gate2_t = keep.tile([P, 2, U], F32, name="gate2_t", tag="w1_raw")
        nc.sync.dma_start(out=gate2_t[:], in_=gate2.rearrange("d p r -> p d r"))

        def gather_term(term, t, d, first, last):
            nc.vector.tensor_tensor(
                term, h[t][:].indirect(pos[d][:, first * BLOCK : last * BLOCK]),
                gate_t[:, d, first * P : last * P], ALU.mult,
            )

        split_cols = SPLIT * P
        terms = [keep.tile([P, PACK, V], F32, name="terms%d" % d) for d in range(2)]

        turned = [bank("turned%d" % b, 6 + b, [P, 2, P]) for b in range(SPLIT)]
        for t in range(2):
            for d in range(2):
                gather_term(terms[d][:, t, :], t, d, 0, PACK)
            for b in range(SPLIT):
                for d in range(2):
                    nc.tensor.matmul(
                        turned[b][:, t, :], terms[d][:, t, b * P : (b + 1) * P], ident[:],
                        start=(d == 0), stop=(d == 1), is_transpose=True,
                    )

        plain = [bank("plain%d" % d, 4 + d, [P, SPLIT, 2, P]) for d in range(2)]
        for d in range(2):
            for e in range(2):
                nc.scalar.activation(
                    terms[d][:, 2 + e, :split_cols], h[2 + e][:].indirect(pos[d][:, : SPLIT * BLOCK]), ACT.Copy
                )
                for b in range(SPLIT):
                    nc.tensor.transpose(plain[d][:, b, e, :], terms[d][:, 2 + e, b * P : (b + 1) * P], ident[:])
        for t in (2, 3):
            for d in range(2):
                gather_term(terms[d][:, t, split_cols:], t, d, SPLIT, PACK)

        woven = [[plain[d][:, b].rearrange("v e p -> v p e") for b in range(SPLIT)] for d in range(2)]
        scaled = []
        for b, tag in enumerate(("zb2", "zb3")):
            first = keep.tile([P, P, 2], F32, name="scaled%d" % b, tag=tag, align_bytes=64)
            nc.scalar.activation(first[:], woven[0][b], ACT.Copy, scale=gate_col[0][:, b : b + 1])
            scaled.append(first)

        back = [bank("back%d" % b, number, [P, 2, P]) for b, number in enumerate((3, 0))]
        for b in range(SPLIT):
            pairs0 = keep.tile([P, P, 2], BF16, name="pairs0%d" % b, align_bytes=64)
            nc.scalar.copy(pairs0[:], turned[b][:].rearrange("v e p -> v p e"))
            nc.tensor.transpose(back[b][:, 0, :], pairs0[:].rearrange("v p e -> v (p e)").bitcast(F32), ident[:])
        zb = []
        for b in range(SPLIT):
            pairs1 = keep.tile([P, P, 2], BF16, name="pairs1%d" % b, align_bytes=64)
            nc.vector.scalar_tensor_tensor(
                pairs1[:], woven[1][b], gate_col[1][:, b : b + 1], scaled[b][:], ALU.mult, ALU.add
            )
            nc.tensor.transpose(back[b][:, 1, :], pairs1[:].rearrange("v p e -> v (p e)").bitcast(F32), ident[:])
            zb_b = keep.tile([P, P * PACK], BF16, name="zb%d" % b, align_bytes=64)
            nc.scalar.copy(zb_b[:].bitcast(F32).rearrange("p (v u) -> p v u", u=2), back[b][:].rearrange("p u v -> p v u"))
            zb.append(zb_b)

        def add_direct(zb_part, start, width):
            views = [terms[d][:, :, start : start + width].rearrange("p t (c i) -> p c t i", i=2) for d in range(2)]
            nc.vector.tensor_tensor(zb_part.rearrange("p (c i t) -> p c t i", i=2, t=PACK), views[0], views[1], ALU.add)

        g = keep.tile([P, V], F32, name="g")

        def second_layer(zb, start, width, tag, number):
            zc = keep.tile([P, width], U32, name="zc%d" % start, tag=tag, align_bytes=64)
            zs = keep.tile([P, width], U8, name="zs%d" % start, align_bytes=64)
            for c in range(0, width, P):
                end = min(c + P, width)
                nc.vector.quantize_mx(
                    out=zc[:, c:end].bitcast(FP8X4), scales=zs[:, c:end], in_=zb[:, PACK * c : PACK * end]
                )
            acc2 = bank("second%d" % start, number, [P, width])
            nc.tensor.matmul_mx(
                out=acc2[:], lhsT=w2w[:].bitcast(FP8X4), lhsT_scale=w2s[:],
                rhs=zc[:].bitcast(FP8X4), rhs_scale=zs[:], start=True, stop=True,
            )
            nc.scalar.activation(g[:, start : start + width], acc2[:], ACT.Relu)

        zb2 = keep.tile([P, P * PACK], BF16, name="zb2", tag="zb2", align_bytes=64)
        zb3 = keep.tile([P, P * PACK], BF16, name="zb3", tag="zb3", align_bytes=64)
        add_direct(zb2[:], 2 * P, P)
        add_direct(zb3[:, : 2 * P], 3 * P, P // 2)
        second_layer(zb2[:], 2 * P, P, "zc2", 5)
        add_direct(zb3[:, 2 * P :], 3 * P + P // 2, P // 2)
        second_layer(zb3[:, : 2 * P], 3 * P, P // 2, "zc30", 6)
        second_layer(zb[0][:], 0, P, "zc0", 2)
        second_layer(zb3[:, 2 * P :], 3 * P + P // 2, P // 2, "zc31", 7)
        second_layer(zb[1][:], P, P, "zc1", 4)

        plain1 = keep.tile([P, SHARED], F32, name="plain1")
        out0 = keep.tile([P, U], F32, name="out0")
        out1 = keep.tile([P, U], F32, name="out1")
        nc.scalar.activation(plain1[:], g[:].indirect(nxt[1][:, : SHARED // LIST]), ACT.Copy)
        nc.vector.tensor_tensor(out0[:], g[:].indirect(nxt[0][:]), gate2_t[:, 0, :], ALU.mult)
        nc.vector.tensor_tensor(
            out1[:, SHARED:], g[:].indirect(nxt[1][:, SHARED // LIST :]), gate2_t[:, 1, SHARED:], ALU.mult
        )
        nc.vector.tensor_tensor(out1[:, :SHARED], plain1[:], gate2_t[:, 1, :SHARED], ALU.mult)
        res = keep.tile([P, U], F32, name="res")
        for part in (slice(SHARED, U), slice(0, SHARED)):
            nc.vector.tensor_tensor(res[:, part], out0[:, part], out1[:, part], ALU.add)
        nc.sync.dma_start(out=out, in_=res[:])
